import numpy as np
import ml_dtypes


def mxq(x, axis, fmt="e4m3"):
    dtype, down = {"e4m3": (ml_dtypes.float8_e4m3fn, 7), "e5m2": (ml_dtypes.float8_e5m2, 14)}[fmt]
    v = np.moveaxis(np.asarray(x, np.float32).astype(ml_dtypes.bfloat16).astype(np.float64), axis, -1)
    blocks = v.reshape(v.shape[:-1] + (-1, 32))
    amax = np.abs(blocks).max(-1, keepdims=True)
    byte = np.maximum(np.where(amax > 0, np.frexp(amax)[1] - 1 + 127, 0) - down, 1)
    scale = np.exp2(byte - 127.0)
    codes = (blocks / scale).astype(np.float32).astype(dtype).astype(np.float64)
    return np.moveaxis((codes * scale).reshape(v.shape), -1, axis)


WIDE = False


def mx_kscale(k):
    if not WIDE:
        return np.ones(k)
    levels = np.array([10, -10, 5, -5, 0])
    if k % 512:
        return np.exp2(np.random.permutation(np.resize(levels, k // 32))).repeat(32)
    a = np.empty((k // 512, 16))
    for p in range(k // 512):
        a[p, :8] = np.random.permutation(np.resize(levels, 8))
        for g in range(8):
            far = levels[np.abs(levels - a[p, g]) >= 10]
            a[p, g + 8] = far[np.random.randint(len(far))]
    return np.exp2(a.ravel()).repeat(32)


def f64(x):
    return np.asarray(x).astype(np.float64)


def striped(idx):
    return np.tile(idx.reshape(-1, 16).T, (8, 1)).astype(np.uint16)


def unstriped(offs):
    return offs[:16].T.reshape(-1).astype(np.int64)


E2M1 = np.array([0.0, 0.5, 1.0, 1.5, 2.0, 3.0, 4.0, 6.0, -0.0, -0.5, -1.0, -1.5, -2.0, -3.0, -4.0, -6.0])


def pack_weight(w, fmt):
    k, n = w.shape
    w = f64(np.asarray(w, np.float32).astype(ml_dtypes.bfloat16)).reshape(k // 32, 32, n)
    amax = np.abs(w).max(1)
    if fmt == "e4m3":
        byte = np.frexp(amax)[1] - 1 + 127 - 7
    else:
        mant, ex = np.frexp(amax / 6.0)
        byte = np.where(mant > 0.5, ex, ex - 1) + 127
    byte = np.clip(np.where(amax > 0, byte, 1), 1, 254)
    scaled = (w * np.exp2(127.0 - byte)[:, None, :]).reshape(k, n).astype(np.float32)
    by_word = np.ascontiguousarray(scaled.reshape(k // 512, 128, 4, n).transpose(0, 1, 3, 2))
    if fmt == "e4m3":
        words = by_word.astype(ml_dtypes.float8_e4m3fn).view(np.uint8)
    else:
        c = by_word.astype(ml_dtypes.float4_e2m1fn).view(np.uint8) & 0xF
        words = (c[..., 0::2] | (c[..., 1::2] << 4)).reshape(k // 512, 128, 2 * n)
    return np.ascontiguousarray(words), np.ascontiguousarray(byte.astype(np.uint8).reshape(k // 512, 16, n))


def unpack_weight(words, scales, fmt):
    g, _, n = scales.shape
    words = np.ascontiguousarray(words).reshape(g, 128, n, -1)
    if fmt == "e4m3":
        vals = words.view(ml_dtypes.float8_e4m3fn).astype(np.float64)
    else:
        nib = np.empty((g, 128, n, 4), np.uint8)
        nib[..., 0::2] = words & 0xF
        nib[..., 1::2] = words >> 4
        vals = E2M1[nib]
    vals = vals * np.repeat(np.exp2(scales.astype(np.float64) - 127.0), 8, axis=1)[..., None]
    return vals.transpose(0, 1, 3, 2).reshape(g * 512, n)


def gelu(v):
    return 0.5 * v * (1.0 + np.tanh(np.sqrt(2.0 / np.pi) * (v + 0.044715 * v**3)))


K, T, S, H, N, P = 1024, 4096, 1024, 1024, 768, 512


def setup_inputs():
    n = np.random.standard_normal
    s = mx_kscale(K)[:, None]
    u = mx_kscale(H)[:, None]
    d = {}
    d["tab_words"], d["tab_scales"] = pack_weight(n((K, T)) * s, "e2m1")
    d["offs"] = striped(np.random.permutation(T)[:S])
    d["w1"] = (1.6 * n((K, H)) / (s * K ** 0.5)).astype(np.float32)
    d["gain"] = (np.exp(0.3 * n(H)) * u[:, 0]).astype(np.float32)
    d["mid"] = ((0.6 + 0.3 * n(H)) * u[:, 0]).astype(np.float32)
    d["pos1"] = striped(np.random.permutation(S)[:P])
    d["pos2"] = striped(np.random.permutation(S)[:P])
    d["w2_words"], d["w2_scales"] = pack_weight(n((H, N)) / (u * H ** 0.5), "e2m1")
    d["w3"] = (n((H, N)) / (u * H ** 0.5)).astype(np.float32)
    d["cur"] = (0.7 * n((N, P))).astype(np.float32)
    return d


def reference(tab_words, tab_scales, offs, w1, gain, mid, pos1, pos2,
              w2_words, w2_scales, w3, cur):
    v = unpack_weight(tab_words, tab_scales, "e2m1")[:, unstriped(offs)]
    a = mxq(f64(w1), 0, "e4m3").T @ v
    h = f64(gain)[:, None] * (a / (1.0 + np.exp(-a))) - f64(mid)[:, None]
    bow = mxq(h[:, unstriped(pos1)], 0, "e4m3")
    stern = mxq(np.abs(h[:, unstriped(pos2)]), 0, "e4m3")
    w2 = unpack_weight(w2_words, w2_scales, "e2m1")
    yb = w2.T @ bow
    ys = mxq(f64(w3), 0, "e4m3").T @ stern
    return np.minimum(yb, ys) - f64(cur)

@@ -1,0 +1,279 @@
+from contextlib import ExitStack
+
+import concourse.mybir as mybir
+
+K, T, S, H, N, M = 1024, 4096, 1024, 1024, 768, 512
+FLOPS = 2 * K * H * S + 2 * 2 * H * N * M
+
+F32 = mybir.dt.float32
+BF16 = mybir.dt.bfloat16
+I32 = mybir.dt.int32
+U32 = mybir.dt.uint32
+U16 = mybir.dt.uint16
+U8 = mybir.dt.uint8
+FP8X4 = mybir.dt.float8_e4m3fn_x4
+FP4X4 = mybir.dt.float4_e2m1fn_x4
+ACT = mybir.ActivationFunctionType
+ALU = mybir.AluOpType
+
+P = 128
+PACK = 4
+PASS = P * PACK
+BANK = 512
+KP = K // PASS
+HP = H // PASS
+NT = N // P
+HALF = M // 2
+QUARTER = M // 4
+W3_CHUNK = N // 3
+LIVE = 32 - 4 * KP
+
+
+def tile_list_towing_team_scores_kernel(
+    tc, tab_words, tab_scales, offs, w1, gain, mid, pos1, pos2, w2_words, w2_scales, w3, cur, out
+):
+    nc = tc.nc
+    with ExitStack() as ctx:
+        keep = ctx.enter_context(tc.tile_pool(name="keep", bufs=1))
+        ring = ctx.enter_context(tc.tile_pool(name="ring", bufs=2))
+        psum = ctx.enter_context(tc.psum_pool(name="psum", bufs=8))
+
+        def kept(shape, dtype, name):
+            return keep.tile(shape, dtype, name=name, align_bytes=64)
+
+        def staged(shape, dtype, name, slot):
+            return keep.tile(shape, dtype, name=name, tag=slot, align_bytes=64)
+
+        offs_sb = keep.tile([P, S // 16], U16, name="offs_sb")
+        pos1_sb = keep.tile([P, M // 16], U16, name="pos1_sb")
+        pos2_sb = keep.tile([P, M // 16], U16, name="pos2_sb")
+        tab_sc = staged([P, T], U8, "tab_sc", "slot_a")
+        tab_w0 = staged([P, T], U16, "tab_w0", "slot_b")
+        picked_sc = kept([P, S], U8, "picked_sc")
+        v_w = [kept([P, S], U16, f"v_w{a}") for a in range(KP)]
+        v_sc = [kept([P, S], U8, f"v_sc{a}") for a in range(KP)]
+        w1_raw = {}
+        w1_q = [[kept([P, PASS], U32, f"w1_q{a}{b}") for b in range(HP)] for a in range(KP)]
+        w1_sc = [[kept([P, PASS], U8, f"w1_sc{a}{b}") for b in range(HP)] for a in range(KP)]
+        w3_bf = [kept([P, N * PACK], BF16, f"w3_bf{b}") for b in range(HP)]
+        w3_q = [kept([P, N], U32, f"w3_q{b}") for b in range(HP)]
+        w3_sc = [kept([P, N], U8, f"w3_sc{b}") for b in range(HP)]
+        gain_sb = kept([P, HP, PACK], F32, "gain_sb")
+        mid_sb = kept([P, HP, PACK], F32, "mid_sb")
+        yb_sb = [[kept([P, 2 * HALF], F32, f"yb{u}{i}") for i in range(NT // 2)] for u in range(2)]
+        warm = kept([P, 8], F32, "warm")
+        warm_out = kept([P, 8], F32, "warm_out")
+        h = [kept([P, S], F32, f"h{t}") for t in range(PACK)]
+        bow_q = [kept([P, M], U32, f"bow_q{b}") for b in range(HP)]
+        bow_sc = [kept([P, M], U8, f"bow_sc{b}") for b in range(HP)]
+        st_q = [kept([P, M], U32, f"st_q{b}") for b in range(HP)]
+        st_sc = [kept([P, M], U8, f"st_sc{b}") for b in range(HP)]
+
+        nc.gpsimd.memset(warm[:], 0.0)
+        for q in range(4):
+            engine = nc.vector if q < 2 else nc.gpsimd
+            engine.memset(tab_sc[32 * q : 32 * q + LIVE, :].bitcast(I32), 0)
+        nc.scalar.activation(warm_out[:], warm[:], ACT.Silu)
+
+        nc.sync.dma_start(offs_sb[:], offs)
+        for q in range(4):
+            nc.sync.dma_start(
+                tab_sc[32 * q + LIVE : 32 * (q + 1), :].bitcast(I32),
+                tab_scales[:, 4 * q : 4 * q + 4, :].bitcast(I32),
+            )
+        nc.sync.dma_start(tab_w0[:].bitcast(I32), tab_words[0].bitcast(I32))
+
+        def load_w1(a, b, tag):
+            w1_raw[a, b] = staged([P, PACK, PASS], F32, f"w1_raw{a}{b}", tag)
+            rows = w1[PASS * a : PASS * (a + 1), PASS * b : PASS * (b + 1)]
+            nc.sync.dma_start(w1_raw[a, b][:], rows.rearrange("(p j) c -> p j c", j=PACK))
+
+        load_w1(0, 0, "slot_c")
+        load_w1(1, 0, "slot_d")
+        nc.sync.dma_start(gain_sb[:], gain.rearrange("(b p t) -> p b t", b=HP, t=PACK))
+        nc.sync.dma_start(mid_sb[:], mid.rearrange("(b p t) -> p b t", b=HP, t=PACK))
+        nc.sync.dma_start(pos1_sb[:], pos1)
+        nc.sync.dma_start(pos2_sb[:], pos2)
+
+        nc.vector.tensor_copy(picked_sc[:], tab_sc[:].indirect(offs_sb[:]))
+        for a in range(KP):
+            first = LIVE + 4 * a
+            nc.scalar.dma_start(v_sc[a][0 : P - first, :].bitcast(I32), picked_sc[first:P, :].bitcast(I32))
+        tab_w1 = staged([P, T], U16, "tab_w1", "slot_a")
+        nc.sync.dma_start(tab_w1[:].bitcast(I32), tab_words[1].bitcast(I32))
+        nc.vector.tensor_copy(v_w[0][:], tab_w0[:].indirect(offs_sb[:]))
+        load_w1(0, 1, "slot_b")
+
+        def weave_w1(copy, a, b, t0, t1):
+            woven = ring.tile([P, (t1 - t0) * PASS], BF16, name="w1_bf", align_bytes=64, bufs=4)
+            dst = woven[:].rearrange("p (t m j) -> p m j t", m=P, j=PACK)
+            src = w1_raw[a, b][:].rearrange("p j (m t) -> p m j t", t=PACK)
+            copy(dst, src[:, :, :, t0:t1])
+            return woven
+
+        def weave(copy, dst, src):
+            copy(
+                dst.rearrange("p (c i j) -> p c j i", i=PACK, j=PACK),
+                src.rearrange("p j (c i) -> p c j i", i=PACK),
+            )
+
+        def quantize(codes, scales, values):
+            nc.vector.quantize_mx(out=codes.bitcast(FP8X4), scales=scales, in_=values)
+
+        def quantize_w1(a, b, t0, t1, woven):
+            quantize(w1_q[a][b][:, P * t0 : P * t1], w1_sc[a][b][:, P * t0 : P * t1], woven[:])
+
+        def scalar_abs(dst, src):
+            nc.scalar.activation(dst, src, ACT.Abs)
+
+        def reading(b, t, act):
+            cols = slice(P * t, P * (t + 1))
+            for j0 in range(0, S, BANK):
+                acc = psum.tile([P, BANK], F32, name="acc")
+                for a in range(KP):
+                    nc.tensor.matmul_mx(
+                        out=acc[:],
+                        lhsT=w1_q[a][b][:, cols].bitcast(FP8X4),
+                        lhsT_scale=w1_sc[a][b][:, cols],
+                        rhs=v_w[a][:, j0 : j0 + BANK].bitcast(FP4X4),
+                        rhs_scale=v_sc[a][:, j0 : j0 + BANK],
+                        start=(a == 0),
+                        stop=(a == KP - 1),
+                    )
+                nc.scalar.activation(act[:, j0 : j0 + BANK], acc[:], ACT.Silu)
+            nc.vector.tensor_scalar(
+                h[t][:], act[:], gain_sb[:, b, t : t + 1], mid_sb[:, b, t : t + 1], ALU.mult, ALU.subtract
+            )
+
+        def pick(dst, t, offsets):
+            nc.vector.tensor_copy(dst[:, t, :], h[t][:].indirect(offsets))
+
+        def w3_part(b, c):
+            n0, n1 = W3_CHUNK * c, W3_CHUNK * (c + 1)
+            weave(nc.scalar.copy, w3_bf[b][:, PACK * n0 : PACK * n1], w3_raw[b][:, :, n0:n1])
+            quantize(w3_q[b][:, n0:n1], w3_sc[b][:, n0:n1], w3_bf[b][:, PACK * n0 : PACK * n1])
+
+        def weave_teams(copy, picked, codes, scales, tag):
+            woven = keep.tile([P, picked.shape[2] * PACK], BF16, name="woven", tag=tag, align_bytes=64)
+            weave(copy, woven[:], picked)
+            quantize(codes, scales, woven[:])
+
+        for a in range(KP):
+            low = weave_w1(nc.vector.tensor_copy, a, 0, 0, 2)
+            high = weave_w1(nc.scalar.copy, a, 0, 2, PACK)
+            quantize_w1(a, 0, 0, 2, low)
+            quantize_w1(a, 0, 2, PACK, high)
+        load_w1(1, 1, "slot_c")
+        for j0 in range(0, S, BANK):
+            listed = offs_sb[:, j0 // 16 : (j0 + BANK) // 16]
+            nc.vector.tensor_copy(v_w[1][:, j0 : j0 + BANK], tab_w1[:].indirect(listed))
+        w3_raw = []
+        for b in range(HP):
+            raw = staged([P, PACK, N], F32, f"w3_raw{b}", ("slot_d", "slot_a")[b])
+            nc.sync.dma_start(raw[:], w3[PASS * b : PASS * (b + 1), :].rearrange("(p j) c -> p j c", j=PACK))
+            w3_raw.append(raw)
+
+        bow0_f = kept([P, PACK, M], F32, "bow0_f")
+        st0_f = kept([P, PACK, M], F32, "st0_f")
+        for t in range(PACK):
+            reading(0, t, ring.tile([P, S], F32, name="act"))
+            pick(bow0_f, t, pos1_sb[:])
+            pick(st0_f, t, pos2_sb[:])
+            if t in (1, 2):
+                quantize_w1(t - 1, 1, 0, PACK, weave_w1(nc.scalar.copy, t - 1, 1, 0, PACK))
+        for c in range(3):
+            w3_part(0, c)
+        w2_w = staged([P, HP, 2 * N], U8, "w2_w", "slot_c")
+        w2_sc = keep.tile([P, HP, N], U8, name="w2_sc", tag="picked_sc", align_bytes=64)
+        nc.sync.dma_start(w2_w[:].bitcast(I32), w2_words.rearrange("b p c -> p b c").bitcast(I32))
+        for q in range(4):
+            nc.sync.dma_start(
+                w2_sc[32 * q : 32 * q + 4, :, :].bitcast(I32),
+                w2_scales[:, 4 * q : 4 * q + 4, :].rearrange("b r c -> r b c").bitcast(I32),
+            )
+        cur_sb = staged([P, NT, M], F32, "cur_sb", "slot_b")
+        nc.sync.dma_start(cur_sb[:], cur.rearrange("(i p) m -> p i m", p=P))
+
+        def offsets(pos_sb, u):
+            return pos_sb[:, HALF // 16 * u : HALF // 16 * (u + 1)]
+
+        bow1_f = kept([P, PACK, HALF], F32, "bow1_f")
+        st1_f = kept([P, PACK, HALF], F32, "st1_f")
+        for t in range(PACK):
+            if t < PACK - 1:
+                act = ring.tile([P, S], F32, name="act")
+            else:
+                act = keep.tile([P, S], F32, name="last_act", tag="second")
+            reading(1, t, act)
+            pick(bow1_f, t, offsets(pos1_sb, 0))
+            pick(st1_f, t, offsets(pos2_sb, 0))
+            if t == 0:
+                w3_part(1, 0)
+            if t == 1:
+                weave_teams(nc.scalar.copy, bow0_f[:], bow_q[0][:], bow_sc[0][:], "bow0_bf")
+            if t == 2:
+                weave_teams(scalar_abs, st0_f[:], st_q[0][:], st_sc[0][:], "st0_bf")
+        w3_part(1, 1)
+        w3_part(1, 2)
+        bow2_f = keep.tile([P, PACK, HALF], F32, name="bow2_f", tag="second")
+        for t in range(PACK):
+            pick(bow2_f, t, offsets(pos1_sb, 1))
+
+        def bow_scores(u):
+            for i0 in range(0, NT, 2):
+                acc = psum.tile([P, BANK], F32, name="acc")
+                for b in range(HP):
+                    for e in range(2):
+                        i = i0 + e
+                        for m0 in range(0, HALF, QUARTER):
+                            teams = slice(HALF * u + m0, HALF * u + m0 + QUARTER)
+                            nc.tensor.matmul_mx(
+                                out=acc[:, HALF * e + m0 : HALF * e + m0 + QUARTER],
+                                lhsT=w2_w[:, b, 2 * P * i : 2 * P * (i + 1)].bitcast(FP4X4),
+                                lhsT_scale=w2_sc[:, b, P * i : P * (i + 1)],
+                                rhs=bow_q[b][:, teams].bitcast(FP8X4),
+                                rhs_scale=bow_sc[b][:, teams],
+                                start=(b == 0 and e == 0 and m0 == 0),
+                                stop=(b == HP - 1 and e == 1 and m0 == QUARTER),
+                            )
+                nc.scalar.copy(yb_sb[u][i0 // 2][:], acc[:])
+
+        out_rows = out.rearrange("(i p) m -> p i m", p=P)
+
+        def finish(u, subtract):
+            teams = slice(HALF * u, HALF * (u + 1))
+            for i0 in range(0, NT, 2):
+                acc = psum.tile([P, BANK], F32, name="acc")
+                for b in range(HP):
+                    for e in range(2):
+                        cols = slice(P * (i0 + e), P * (i0 + e + 1))
+                        nc.tensor.matmul_mx(
+                            out=acc[:, HALF * e : HALF * (e + 1)],
+                            lhsT=w3_q[b][:, cols].bitcast(FP8X4),
+                            lhsT_scale=w3_sc[b][:, cols],
+                            rhs=st_q[b][:, teams].bitcast(FP8X4),
+                            rhs_scale=st_sc[b][:, teams],
+                            start=(b == 0 and e == 0),
+                            stop=(b == HP - 1 and e == 1),
+                        )
+                weaker = yb_sb[u][i0 // 2][:]
+                nc.vector.tensor_tensor(weaker, acc[:], weaker, ALU.min)
+                res = weaker.rearrange("p (e m) -> p e m", e=2)
+                subtract(res, res, cur_sb[:, i0 : i0 + 2, teams], ALU.subtract)
+                nc.sync.dma_start(out_rows[:, i0 : i0 + 2, teams], res)
+
+        def weave_half(copy, picked, codes, scales, u, tag):
+            teams = slice(HALF * u, HALF * (u + 1))
+            weave_teams(copy, picked, codes[1][:, teams], scales[1][:, teams], tag)
+
+        weave_half(nc.scalar.copy, bow1_f[:], bow_q, bow_sc, 0, "bow1_bf")
+        weave_half(scalar_abs, st1_f[:], st_q, st_sc, 0, "st1_bf")
+        st2_f = keep.tile([P, PACK, HALF], F32, name="st2_f", tag="st1_bf", align_bytes=64)
+        for t in range(PACK):
+            pick(st2_f, t, offsets(pos2_sb, 1))
+        weave_half(nc.scalar.copy, bow2_f[:], bow_q, bow_sc, 1, "bow2_bf")
+        bow_scores(0)
+        weave_half(scalar_abs, st2_f[:], st_q, st_sc, 1, "st2_bf")
+        finish(0, nc.vector.tensor_tensor)
+        bow_scores(1)
+        finish(1, nc.vector.tensor_tensor)

@@ -25,8 +25,10 @@ HP = H // PASS
 NT = N // P
 HALF = M // 2
 QUARTER = M // 4
-W3_CHUNK = N // 3
-LIVE = 32 - 4 * KP
+DEAD = 32 - 4 * KP
+W3_CHUNK = 256
+W3_SPLIT = 1024
+STAGE1_BANKS = 4
 
 
 def tile_list_towing_team_scores_kernel(
@@ -35,61 +37,61 @@ def tile_list_towing_team_scores_kernel(
     nc = tc.nc
     with ExitStack() as ctx:
         keep = ctx.enter_context(tc.tile_pool(name="keep", bufs=1))
-        ring = ctx.enter_context(tc.tile_pool(name="ring", bufs=2))
-        psum = ctx.enter_context(tc.psum_pool(name="psum", bufs=8))
+        psum = ctx.enter_context(tc.psum_pool(name="psum", bufs=1))
 
-        def kept(shape, dtype, name):
-            return keep.tile(shape, dtype, name=name, align_bytes=64)
-
-        def staged(shape, dtype, name, slot):
+        def sbuf(shape, dtype, name, slot=""):
             return keep.tile(shape, dtype, name=name, tag=slot, align_bytes=64)
+
+        def bank(n):
+            return psum.tile([P, BANK], F32, name=f"bank{n}")
 
         offs_sb = keep.tile([P, S // 16], U16, name="offs_sb")
         pos1_sb = keep.tile([P, M // 16], U16, name="pos1_sb")
         pos2_sb = keep.tile([P, M // 16], U16, name="pos2_sb")
-        tab_sc = staged([P, T], U8, "tab_sc", "slot_a")
-        tab_w0 = staged([P, T], U16, "tab_w0", "slot_b")
-        picked_sc = kept([P, S], U8, "picked_sc")
-        v_w = [kept([P, S], U16, f"v_w{a}") for a in range(KP)]
-        v_sc = [kept([P, S], U8, f"v_sc{a}") for a in range(KP)]
+        tab_sc = sbuf([P, T], U8, "tab_sc", "slot_a")
+        tab_w = [sbuf([P, T], U16, f"tab_w{a}", ("slot_b", "slot_c")[a]) for a in range(KP)]
+        picked_sc = sbuf([P, S], U8, "picked_sc")
+        v_w = [sbuf([P, S], U16, f"v_w{a}") for a in range(KP)]
+        v_sc = [sbuf([P, S], U8, f"v_sc{a}") for a in range(KP)]
         w1_raw = {}
-        w1_q = [[kept([P, PASS], U32, f"w1_q{a}{b}") for b in range(HP)] for a in range(KP)]
-        w1_sc = [[kept([P, PASS], U8, f"w1_sc{a}{b}") for b in range(HP)] for a in range(KP)]
-        w3_bf = [kept([P, N * PACK], BF16, f"w3_bf{b}") for b in range(HP)]
-        w3_q = [kept([P, N], U32, f"w3_q{b}") for b in range(HP)]
-        w3_sc = [kept([P, N], U8, f"w3_sc{b}") for b in range(HP)]
-        gain_sb = kept([P, HP, PACK], F32, "gain_sb")
-        mid_sb = kept([P, HP, PACK], F32, "mid_sb")
-        yb_sb = [[kept([P, 2 * HALF], F32, f"yb{u}{i}") for i in range(NT // 2)] for u in range(2)]
-        warm = kept([P, 8], F32, "warm")
-        warm_out = kept([P, 8], F32, "warm_out")
-        h = [kept([P, S], F32, f"h{t}") for t in range(PACK)]
-        bow_q = [kept([P, M], U32, f"bow_q{b}") for b in range(HP)]
-        bow_sc = [kept([P, M], U8, f"bow_sc{b}") for b in range(HP)]
-        st_q = [kept([P, M], U32, f"st_q{b}") for b in range(HP)]
-        st_sc = [kept([P, M], U8, f"st_sc{b}") for b in range(HP)]
+        w1_bf = {(b, g): sbuf([P, KP, 2 * PASS], BF16, f"w1_bf{b}{g}") for b in range(HP) for g in range(2)}
+        w1_q = {(b, g): sbuf([P, KP, 2 * P], U32, f"w1_q{b}{g}") for b in range(HP) for g in range(2)}
+        w1_sc = {(b, g): sbuf([P, KP, 2 * P], U8, f"w1_sc{b}{g}") for b in range(HP) for g in range(2)}
+        w3_bf = sbuf([P, HP * N * PACK], BF16, "w3_bf")
+        w3_q = sbuf([P, HP * N], U32, "w3_q")
+        w3_sc = sbuf([P, HP * N], U8, "w3_sc")
+        gain_sb = sbuf([P, HP, PACK], F32, "gain_sb")
+        mid_sb = sbuf([P, HP, PACK], F32, "mid_sb")
+        warm = sbuf([P, 8], F32, "warm")
+        warm_out = sbuf([P, 8], F32, "warm_out")
+        h = [[sbuf([P, S], F32, f"h{b}{t}") for t in range(PACK)] for b in range(HP)]
+        bow_q = [sbuf([P, M], U32, f"bow_q{b}") for b in range(HP)]
+        bow_sc = [sbuf([P, M], U8, f"bow_sc{b}") for b in range(HP)]
+        st_q = [sbuf([P, M], U32, f"st_q{b}") for b in range(HP)]
+        st_sc = [sbuf([P, M], U8, f"st_sc{b}") for b in range(HP)]
+        scores = [[sbuf([P, 2 * HALF], F32, f"scores{u}{i}") for i in range(NT // 2)] for u in range(2)]
 
         nc.gpsimd.memset(warm[:], 0.0)
         for q in range(4):
             engine = nc.vector if q < 2 else nc.gpsimd
-            engine.memset(tab_sc[32 * q : 32 * q + LIVE, :].bitcast(I32), 0)
+            engine.memset(tab_sc[32 * q : 32 * q + DEAD, :].bitcast(I32), 0)
         nc.scalar.activation(warm_out[:], warm[:], ACT.Silu)
 
         nc.sync.dma_start(offs_sb[:], offs)
         for q in range(4):
             nc.sync.dma_start(
-                tab_sc[32 * q + LIVE : 32 * (q + 1), :].bitcast(I32),
+                tab_sc[32 * q + DEAD : 32 * (q + 1), :].bitcast(I32),
                 tab_scales[:, 4 * q : 4 * q + 4, :].bitcast(I32),
             )
-        nc.sync.dma_start(tab_w0[:].bitcast(I32), tab_words[0].bitcast(I32))
+        for a in range(KP):
+            nc.sync.dma_start(tab_w[a][:].bitcast(I32), tab_words[a].bitcast(I32))
 
-        def load_w1(a, b, tag):
-            w1_raw[a, b] = staged([P, PACK, PASS], F32, f"w1_raw{a}{b}", tag)
+        def load_w1(a, b, slot):
+            w1_raw[a, b] = sbuf([P, PACK, PASS], F32, f"w1_raw{a}{b}", slot)
             rows = w1[PASS * a : PASS * (a + 1), PASS * b : PASS * (b + 1)]
             nc.sync.dma_start(w1_raw[a, b][:], rows.rearrange("(p j) c -> p j c", j=PACK))
 
-        load_w1(0, 0, "slot_c")
-        load_w1(1, 0, "slot_d")
+        load_w1(0, 0, "slot_d")
         nc.sync.dma_start(gain_sb[:], gain.rearrange("(b p t) -> p b t", b=HP, t=PACK))
         nc.sync.dma_start(mid_sb[:], mid.rearrange("(b p t) -> p b t", b=HP, t=PACK))
         nc.sync.dma_start(pos1_sb[:], pos1)
@@ -97,19 +99,29 @@ def tile_list_towing_team_scores_kernel(
 
         nc.vector.tensor_copy(picked_sc[:], tab_sc[:].indirect(offs_sb[:]))
         for a in range(KP):
-            first = LIVE + 4 * a
+            first = DEAD + 4 * a
             nc.scalar.dma_start(v_sc[a][0 : P - first, :].bitcast(I32), picked_sc[first:P, :].bitcast(I32))
-        tab_w1 = staged([P, T], U16, "tab_w1", "slot_a")
-        nc.sync.dma_start(tab_w1[:].bitcast(I32), tab_words[1].bitcast(I32))
-        nc.vector.tensor_copy(v_w[0][:], tab_w0[:].indirect(offs_sb[:]))
-        load_w1(0, 1, "slot_b")
+        load_w1(1, 0, "slot_a")
+        for a in range(KP):
+            nc.vector.tensor_copy(v_w[a][:], tab_w[a][:].indirect(offs_sb[:]))
+            load_w1(a, 1, ("slot_b", "slot_c")[a])
 
-        def weave_w1(copy, a, b, t0, t1):
-            woven = ring.tile([P, (t1 - t0) * PASS], BF16, name="w1_bf", align_bytes=64, bufs=4)
-            dst = woven[:].rearrange("p (t m j) -> p m j t", m=P, j=PACK)
+        def quantize(codes, scales, values):
+            nc.vector.quantize_mx(out=codes.bitcast(FP8X4), scales=scales, in_=values)
+
+        def weave_w1(copy, a, b, g):
+            dst = w1_bf[b, g][:, a, :].rearrange("p (t m j) -> p m j t", m=P, j=PACK)
             src = w1_raw[a, b][:].rearrange("p j (m t) -> p m j t", t=PACK)
-            copy(dst, src[:, :, :, t0:t1])
-            return woven
+            copy(dst, src[:, :, :, 2 * g : 2 * g + 2])
+
+        def quantize_w1_pass(a, b, g):
+            quantize(w1_q[b, g][:, a, :], w1_sc[b, g][:, a, :], w1_bf[b, g][:, a, :])
+
+        def both_passes_w1(b, g):
+            for a in range(KP):
+                weave_w1(nc.scalar.copy, a, b, g)
+            flat = "p a c -> p (a c)"
+            quantize(w1_q[b, g][:].rearrange(flat), w1_sc[b, g][:].rearrange(flat), w1_bf[b, g][:].rearrange(flat))
 
         def weave(copy, dst, src):
             copy(
@@ -117,111 +129,99 @@ def tile_list_towing_team_scores_kernel(
                 src.rearrange("p j (c i) -> p c j i", i=PACK),
             )
 
-        def quantize(codes, scales, values):
-            nc.vector.quantize_mx(out=codes.bitcast(FP8X4), scales=scales, in_=values)
-
-        def quantize_w1(a, b, t0, t1, woven):
-            quantize(w1_q[a][b][:, P * t0 : P * t1], w1_sc[a][b][:, P * t0 : P * t1], woven[:])
-
         def scalar_abs(dst, src):
             nc.scalar.activation(dst, src, ACT.Abs)
 
-        def reading(b, t, act):
-            cols = slice(P * t, P * (t + 1))
-            for j0 in range(0, S, BANK):
-                acc = psum.tile([P, BANK], F32, name="acc")
+        def reading(b, t, act, affine):
+            g, cols = t // 2, slice(P * (t % 2), P * (t % 2 + 1))
+            for jb in range(S // BANK):
+                listed = slice(BANK * jb, BANK * (jb + 1))
+                acc = bank((2 * t + jb) % STAGE1_BANKS)
                 for a in range(KP):
                     nc.tensor.matmul_mx(
                         out=acc[:],
-                        lhsT=w1_q[a][b][:, cols].bitcast(FP8X4),
-                        lhsT_scale=w1_sc[a][b][:, cols],
-                        rhs=v_w[a][:, j0 : j0 + BANK].bitcast(FP4X4),
-                        rhs_scale=v_sc[a][:, j0 : j0 + BANK],
+                        lhsT=w1_q[b, g][:, a, cols].bitcast(FP8X4),
+                        lhsT_scale=w1_sc[b, g][:, a, cols],
+                        rhs=v_w[a][:, listed].bitcast(FP4X4),
+                        rhs_scale=v_sc[a][:, listed],
                         start=(a == 0),
                         stop=(a == KP - 1),
                     )
-                nc.scalar.activation(act[:, j0 : j0 + BANK], acc[:], ACT.Silu)
-            nc.vector.tensor_scalar(
-                h[t][:], act[:], gain_sb[:, b, t : t + 1], mid_sb[:, b, t : t + 1], ALU.mult, ALU.subtract
-            )
+                nc.scalar.activation(act[:, listed], acc[:], ACT.Silu)
+            affine(h[b][t][:], act[:], gain_sb[:, b, t : t + 1], mid_sb[:, b, t : t + 1], ALU.mult, ALU.subtract)
 
-        def pick(dst, t, offsets):
-            nc.vector.tensor_copy(dst[:, t, :], h[t][:].indirect(offsets))
+        def pick(dst, b, t, offsets):
+            nc.vector.tensor_copy(dst[:, t, :], h[b][t][:].indirect(offsets))
 
-        def w3_part(b, c):
-            n0, n1 = W3_CHUNK * c, W3_CHUNK * (c + 1)
-            weave(nc.scalar.copy, w3_bf[b][:, PACK * n0 : PACK * n1], w3_raw[b][:, :, n0:n1])
-            quantize(w3_q[b][:, n0:n1], w3_sc[b][:, n0:n1], w3_bf[b][:, PACK * n0 : PACK * n1])
-
-        def weave_teams(copy, picked, codes, scales, tag):
-            woven = keep.tile([P, picked.shape[2] * PACK], BF16, name="woven", tag=tag, align_bytes=64)
+        def weave_teams(copy, picked, codes, scales, slot):
+            woven = sbuf([P, picked.shape[2] * PACK], BF16, "woven", slot)
             weave(copy, woven[:], picked)
             quantize(codes, scales, woven[:])
 
-        for a in range(KP):
-            low = weave_w1(nc.vector.tensor_copy, a, 0, 0, 2)
-            high = weave_w1(nc.scalar.copy, a, 0, 2, PACK)
-            quantize_w1(a, 0, 0, 2, low)
-            quantize_w1(a, 0, 2, PACK, high)
-        load_w1(1, 1, "slot_c")
-        for j0 in range(0, S, BANK):
-            listed = offs_sb[:, j0 // 16 : (j0 + BANK) // 16]
-            nc.vector.tensor_copy(v_w[1][:, j0 : j0 + BANK], tab_w1[:].indirect(listed))
+        weave_w1(nc.scalar.copy, 0, 0, 0)
+        quantize_w1_pass(0, 0, 0)
+        weave_w1(nc.scalar.copy, 0, 0, 1)
+        weave_w1(nc.vector.tensor_copy, 1, 0, 0)
+        quantize_w1_pass(1, 0, 0)
+        weave_w1(nc.scalar.copy, 1, 0, 1)
+        quantize_w1_pass(0, 0, 1)
+        quantize_w1_pass(1, 0, 1)
         w3_raw = []
         for b in range(HP):
-            raw = staged([P, PACK, N], F32, f"w3_raw{b}", ("slot_d", "slot_a")[b])
+            raw = sbuf([P, PACK, N], F32, f"w3_raw{b}", ("slot_d", "slot_a")[b])
             nc.sync.dma_start(raw[:], w3[PASS * b : PASS * (b + 1), :].rearrange("(p j) c -> p j c", j=PACK))
             w3_raw.append(raw)
 
-        bow0_f = kept([P, PACK, M], F32, "bow0_f")
-        st0_f = kept([P, PACK, M], F32, "st0_f")
+        bow0_f = sbuf([P, PACK, M], F32, "bow0_f")
+        st0_f = sbuf([P, PACK, M], F32, "st0_f")
         for t in range(PACK):
-            reading(0, t, ring.tile([P, S], F32, name="act"))
-            pick(bow0_f, t, pos1_sb[:])
-            pick(st0_f, t, pos2_sb[:])
-            if t in (1, 2):
-                quantize_w1(t - 1, 1, 0, PACK, weave_w1(nc.scalar.copy, t - 1, 1, 0, PACK))
-        for c in range(3):
-            w3_part(0, c)
-        w2_w = staged([P, HP, 2 * N], U8, "w2_w", "slot_c")
-        w2_sc = keep.tile([P, HP, N], U8, name="w2_sc", tag="picked_sc", align_bytes=64)
+            act = sbuf([P, S], F32, f"act0{t}", f"act{t % 3}")
+            reading(0, t, act, nc.vector.tensor_scalar if t == 0 else nc.gpsimd.tensor_scalar)
+            pick(bow0_f, 0, t, pos1_sb[:])
+            pick(st0_f, 0, t, pos2_sb[:])
+            if t % 2 == 1:
+                both_passes_w1(1, t // 2)
+
+        w2_w = sbuf([P, HP, 2 * N], U8, "w2_w", "slot_c")
+        w2_sc = sbuf([P, HP, N], U8, "w2_sc", "picked_sc")
         nc.sync.dma_start(w2_w[:].bitcast(I32), w2_words.rearrange("b p c -> p b c").bitcast(I32))
         for q in range(4):
             nc.sync.dma_start(
                 w2_sc[32 * q : 32 * q + 4, :, :].bitcast(I32),
                 w2_scales[:, 4 * q : 4 * q + 4, :].rearrange("b r c -> r b c").bitcast(I32),
             )
-        cur_sb = staged([P, NT, M], F32, "cur_sb", "slot_b")
+        cur_sb = sbuf([P, NT, M], F32, "cur_sb", "slot_b")
         nc.sync.dma_start(cur_sb[:], cur.rearrange("(i p) m -> p i m", p=P))
 
         def offsets(pos_sb, u):
             return pos_sb[:, HALF // 16 * u : HALF // 16 * (u + 1)]
 
-        bow1_f = kept([P, PACK, HALF], F32, "bow1_f")
-        st1_f = kept([P, PACK, HALF], F32, "st1_f")
+        bow1_f = sbuf([P, PACK, HALF], F32, "bow1_f")
+        st1_f = sbuf([P, PACK, HALF], F32, "st1_f")
         for t in range(PACK):
-            if t < PACK - 1:
-                act = ring.tile([P, S], F32, name="act")
-            else:
-                act = keep.tile([P, S], F32, name="last_act", tag="second")
-            reading(1, t, act)
-            pick(bow1_f, t, offsets(pos1_sb, 0))
-            pick(st1_f, t, offsets(pos2_sb, 0))
-            if t == 0:
-                w3_part(1, 0)
-            if t == 1:
-                weave_teams(nc.scalar.copy, bow0_f[:], bow_q[0][:], bow_sc[0][:], "bow0_bf")
-            if t == 2:
-                weave_teams(scalar_abs, st0_f[:], st_q[0][:], st_sc[0][:], "st0_bf")
-        w3_part(1, 1)
-        w3_part(1, 2)
-        bow2_f = keep.tile([P, PACK, HALF], F32, name="bow2_f", tag="second")
+            act = sbuf([P, S], F32, f"act1{t}", ("act1", "bow0_bf", "st0_bf", "bow2_f")[t])
+            reading(1, t, act, nc.gpsimd.tensor_scalar)
+            pick(bow1_f, 1, t, offsets(pos1_sb, 0))
+            pick(st1_f, 1, t, offsets(pos2_sb, 0))
+        weave_teams(nc.scalar.copy, bow0_f[:], bow_q[0][:], bow_sc[0][:], "bow0_bf")
+        weave_teams(scalar_abs, st0_f[:], st_q[0][:], st_sc[0][:], "st0_bf")
+        for c in range(HP * N // W3_CHUNK):
+            b, n0 = divmod(W3_CHUNK * c, N)
+            woven = w3_bf[:, PACK * W3_CHUNK * c : PACK * W3_CHUNK * (c + 1)]
+            nc.gpsimd.tensor_scalar(
+                woven.rearrange("p (n j) -> p n j", j=PACK),
+                w3_raw[b][:, :, n0 : n0 + W3_CHUNK].rearrange("p j n -> p n j"),
+                1.0, 0.0, ALU.mult, ALU.add,
+            )
+        quantize(w3_q[:, :W3_SPLIT], w3_sc[:, :W3_SPLIT], w3_bf[:, : PACK * W3_SPLIT])
+        quantize(w3_q[:, W3_SPLIT:], w3_sc[:, W3_SPLIT:], w3_bf[:, PACK * W3_SPLIT :])
+        bow2_f = sbuf([P, PACK, HALF], F32, "bow2_f")
         for t in range(PACK):
-            pick(bow2_f, t, offsets(pos1_sb, 1))
+            pick(bow2_f, 1, t, offsets(pos1_sb, 1))
 
-        def bow_scores(u):
+        def bow_scores(u, banks):
             for i0 in range(0, NT, 2):
-                acc = psum.tile([P, BANK], F32, name="acc")
+                acc = bank(banks[i0 // 2])
                 for b in range(HP):
                     for e in range(2):
                         i = i0 + e
@@ -236,44 +236,44 @@ def tile_list_towing_team_scores_kernel(
                                 start=(b == 0 and e == 0 and m0 == 0),
                                 stop=(b == HP - 1 and e == 1 and m0 == QUARTER),
                             )
-                nc.scalar.copy(yb_sb[u][i0 // 2][:], acc[:])
+                nc.scalar.copy(scores[u][i0 // 2][:], acc[:])
 
         out_rows = out.rearrange("(i p) m -> p i m", p=P)
 
-        def finish(u, subtract):
+        def finish(u, banks, subtract):
             teams = slice(HALF * u, HALF * (u + 1))
             for i0 in range(0, NT, 2):
-                acc = psum.tile([P, BANK], F32, name="acc")
+                acc = bank(banks[i0 // 2])
                 for b in range(HP):
                     for e in range(2):
-                        cols = slice(P * (i0 + e), P * (i0 + e + 1))
+                        cols = slice(N * b + P * (i0 + e), N * b + P * (i0 + e + 1))
                         nc.tensor.matmul_mx(
                             out=acc[:, HALF * e : HALF * (e + 1)],
-                            lhsT=w3_q[b][:, cols].bitcast(FP8X4),
-                            lhsT_scale=w3_sc[b][:, cols],
+                            lhsT=w3_q[:, cols].bitcast(FP8X4),
+                            lhsT_scale=w3_sc[:, cols],
                             rhs=st_q[b][:, teams].bitcast(FP8X4),
                             rhs_scale=st_sc[b][:, teams],
                             start=(b == 0 and e == 0),
                             stop=(b == HP - 1 and e == 1),
                         )
-                weaker = yb_sb[u][i0 // 2][:]
+                weaker = scores[u][i0 // 2][:]
                 nc.vector.tensor_tensor(weaker, acc[:], weaker, ALU.min)
                 res = weaker.rearrange("p (e m) -> p e m", e=2)
                 subtract(res, res, cur_sb[:, i0 : i0 + 2, teams], ALU.subtract)
                 nc.sync.dma_start(out_rows[:, i0 : i0 + 2, teams], res)
 
-        def weave_half(copy, picked, codes, scales, u, tag):
+        def weave_half(copy, picked, codes, scales, u, slot):
             teams = slice(HALF * u, HALF * (u + 1))
-            weave_teams(copy, picked, codes[1][:, teams], scales[1][:, teams], tag)
+            weave_teams(copy, picked, codes[1][:, teams], scales[1][:, teams], slot)
 
         weave_half(nc.scalar.copy, bow1_f[:], bow_q, bow_sc, 0, "bow1_bf")
-        weave_half(scalar_abs, st1_f[:], st_q, st_sc, 0, "st1_bf")
-        st2_f = keep.tile([P, PACK, HALF], F32, name="st2_f", tag="st1_bf", align_bytes=64)
+        weave_half(scalar_abs, st1_f[:], st_q, st_sc, 0, "st2_f")
+        st2_f = sbuf([P, PACK, HALF], F32, "st2_f")
         for t in range(PACK):
-            pick(st2_f, t, offsets(pos2_sb, 1))
+            pick(st2_f, 1, t, offsets(pos2_sb, 1))
         weave_half(nc.scalar.copy, bow2_f[:], bow_q, bow_sc, 1, "bow2_bf")
-        bow_scores(0)
+        bow_scores(0, (4, 5, 6))
         weave_half(scalar_abs, st2_f[:], st_q, st_sc, 1, "st2_bf")
-        finish(0, nc.vector.tensor_tensor)
-        bow_scores(1)
-        finish(1, nc.vector.tensor_tensor)
+        finish(0, (7, 0, 1), nc.gpsimd.tensor_tensor)
+        bow_scores(1, (2, 3, 4))
+        finish(1, (5, 6, 7), nc.vector.tensor_tensor)

@@ -23,12 +23,12 @@ BANK = 512
 KP = K // PASS
 HP = H // PASS
 NT = N // P
-HALF = M // 2
-QUARTER = M // 4
 DEAD = 32 - 4 * KP
 W3_CHUNK = 256
+W3_ON_VECTOR = 1
 W3_SPLIT = 1024
 STAGE1_BANKS = 4
+SUBTRACT_ON_GPSIMD = 2
 
 
 def tile_list_towing_team_scores_kernel(
@@ -49,7 +49,7 @@ def tile_list_towing_team_scores_kernel(
         pos1_sb = keep.tile([P, M // 16], U16, name="pos1_sb")
         pos2_sb = keep.tile([P, M // 16], U16, name="pos2_sb")
         tab_sc = sbuf([P, T], U8, "tab_sc", "slot_a")
-        tab_w = [sbuf([P, T], U16, f"tab_w{a}", ("slot_b", "slot_c")[a]) for a in range(KP)]
+        tab_w0 = sbuf([P, T], U16, "tab_w0", "slot_b")
         picked_sc = sbuf([P, S], U8, "picked_sc")
         v_w = [sbuf([P, S], U16, f"v_w{a}") for a in range(KP)]
         v_sc = [sbuf([P, S], U8, f"v_sc{a}") for a in range(KP)]
@@ -60,16 +60,17 @@ def tile_list_towing_team_scores_kernel(
         w3_bf = sbuf([P, HP * N * PACK], BF16, "w3_bf")
         w3_q = sbuf([P, HP * N], U32, "w3_q")
         w3_sc = sbuf([P, HP * N], U8, "w3_sc")
-        gain_sb = sbuf([P, HP, PACK], F32, "gain_sb")
-        mid_sb = sbuf([P, HP, PACK], F32, "mid_sb")
+        minus_mid = sbuf([P, HP, PACK], F32, "minus_mid")
         warm = sbuf([P, 8], F32, "warm")
         warm_out = sbuf([P, 8], F32, "warm_out")
-        h = [[sbuf([P, S], F32, f"h{b}{t}") for t in range(PACK)] for b in range(HP)]
-        bow_q = [sbuf([P, M], U32, f"bow_q{b}") for b in range(HP)]
-        bow_sc = [sbuf([P, M], U8, f"bow_sc{b}") for b in range(HP)]
-        st_q = [sbuf([P, M], U32, f"st_q{b}") for b in range(HP)]
-        st_sc = [sbuf([P, M], U8, f"st_sc{b}") for b in range(HP)]
-        scores = [[sbuf([P, 2 * HALF], F32, f"scores{u}{i}") for i in range(NT // 2)] for u in range(2)]
+        ends = ("bow", "stern")
+        lists = {"bow": pos1_sb, "stern": pos2_sb}
+        funcs = {"bow": ACT.Identity, "stern": ACT.Abs}
+        team_q = {(e, b): sbuf([P, M], U32, f"{e}_q{b}") for e in ends for b in range(HP)}
+        team_sc = {(e, b): sbuf([P, M], U8, f"{e}_sc{b}") for e in ends for b in range(HP)}
+        planes = {}
+        picked = {}
+        scores = [sbuf([P, M], F32, f"scores{i}") for i in range(NT)]
 
         nc.gpsimd.memset(warm[:], 0.0)
         for q in range(4):
@@ -83,28 +84,26 @@ def tile_list_towing_team_scores_kernel(
                 tab_sc[32 * q + DEAD : 32 * (q + 1), :].bitcast(I32),
                 tab_scales[:, 4 * q : 4 * q + 4, :].bitcast(I32),
             )
-        for a in range(KP):
-            nc.sync.dma_start(tab_w[a][:].bitcast(I32), tab_words[a].bitcast(I32))
+        nc.sync.dma_start(tab_w0[:].bitcast(I32), tab_words[0].bitcast(I32))
 
         def load_w1(a, b, slot):
             w1_raw[a, b] = sbuf([P, PACK, PASS], F32, f"w1_raw{a}{b}", slot)
             rows = w1[PASS * a : PASS * (a + 1), PASS * b : PASS * (b + 1)]
             nc.sync.dma_start(w1_raw[a, b][:], rows.rearrange("(p j) c -> p j c", j=PACK))
 
-        load_w1(0, 0, "slot_d")
-        nc.sync.dma_start(gain_sb[:], gain.rearrange("(b p t) -> p b t", b=HP, t=PACK))
-        nc.sync.dma_start(mid_sb[:], mid.rearrange("(b p t) -> p b t", b=HP, t=PACK))
+        load_w1(0, 0, "slot_c")
+        load_w1(1, 0, "slot_d")
         nc.sync.dma_start(pos1_sb[:], pos1)
         nc.sync.dma_start(pos2_sb[:], pos2)
 
         nc.vector.tensor_copy(picked_sc[:], tab_sc[:].indirect(offs_sb[:]))
         for a in range(KP):
             first = DEAD + 4 * a
-            nc.scalar.dma_start(v_sc[a][0 : P - first, :].bitcast(I32), picked_sc[first:P, :].bitcast(I32))
-        load_w1(1, 0, "slot_a")
-        for a in range(KP):
-            nc.vector.tensor_copy(v_w[a][:], tab_w[a][:].indirect(offs_sb[:]))
-            load_w1(a, 1, ("slot_b", "slot_c")[a])
+            nc.sync.dma_start(v_sc[a][0 : P - first, :].bitcast(I32), picked_sc[first:P, :].bitcast(I32))
+        tab_w1 = sbuf([P, T], U16, "tab_w1", "slot_a")
+        nc.sync.dma_start(tab_w1[:].bitcast(I32), tab_words[1].bitcast(I32))
+        nc.vector.tensor_copy(v_w[0][:], tab_w0[:].indirect(offs_sb[:]))
+        load_w1(0, 1, "slot_b")
 
         def quantize(codes, scales, values):
             nc.vector.quantize_mx(out=codes.bitcast(FP8X4), scales=scales, in_=values)
@@ -117,9 +116,7 @@ def tile_list_towing_team_scores_kernel(
         def quantize_w1_pass(a, b, g):
             quantize(w1_q[b, g][:, a, :], w1_sc[b, g][:, a, :], w1_bf[b, g][:, a, :])
 
-        def both_passes_w1(b, g):
-            for a in range(KP):
-                weave_w1(nc.scalar.copy, a, b, g)
+        def quantize_w1_both(b, g):
             flat = "p a c -> p (a c)"
             quantize(w1_q[b, g][:].rearrange(flat), w1_sc[b, g][:].rearrange(flat), w1_bf[b, g][:].rearrange(flat))
 
@@ -129,11 +126,9 @@ def tile_list_towing_team_scores_kernel(
                 src.rearrange("p j (c i) -> p c j i", i=PACK),
             )
 
-        def scalar_abs(dst, src):
-            nc.scalar.activation(dst, src, ACT.Abs)
-
-        def reading(b, t, act, affine):
+        def reading(b, t):
             g, cols = t // 2, slice(P * (t % 2), P * (t % 2 + 1))
+            act = sbuf([P, S], F32, f"act{b}{t}", f"act{(PACK * b + t) % 4}")
             for jb in range(S // BANK):
                 listed = slice(BANK * jb, BANK * (jb + 1))
                 acc = bank((2 * t + jb) % STAGE1_BANKS)
@@ -148,39 +143,61 @@ def tile_list_towing_team_scores_kernel(
                         stop=(a == KP - 1),
                     )
                 nc.scalar.activation(act[:, listed], acc[:], ACT.Silu)
-            affine(h[b][t][:], act[:], gain_sb[:, b, t : t + 1], mid_sb[:, b, t : t + 1], ALU.mult, ALU.subtract)
+            for e in ends:
+                slot = "w1_bf10" if (e, b, t) == ("stern", 0, 2) else ""
+                picked[e, b, t] = sbuf([P, M], F32, f"{e}_picked{b}{t}", slot)
+                nc.vector.tensor_copy(picked[e, b, t][:], act[:].indirect(lists[e][:]))
 
-        def pick(dst, b, t, offsets):
-            nc.vector.tensor_copy(dst[:, t, :], h[b][t][:].indirect(offsets))
+        def rounded(e, b, ts):
+            planes[e, b] = sbuf([P, PACK, M], BF16, f"{e}_planes{b}", f"act{ends.index(e)}" if b == 0 else "")
+            for t in ts:
+                nc.scalar.activation(
+                    planes[e, b][:, t, :], picked[e, b, t][:], funcs[e],
+                    bias=minus_mid[:, b, t : t + 1], scale=gain_sb[:, b, t : t + 1],
+                )
 
-        def weave_teams(copy, picked, codes, scales, slot):
-            woven = sbuf([P, picked.shape[2] * PACK], BF16, "woven", slot)
-            weave(copy, woven[:], picked)
-            quantize(codes, scales, woven[:])
+        def quantize_teams(e, b, slot=""):
+            woven = sbuf([P, M * PACK], BF16, f"{e}_woven{b}", slot)
+            weave(nc.vector.tensor_copy, woven[:], planes[e, b][:])
+            quantize(team_q[e, b][:], team_sc[e, b][:], woven[:])
 
-        weave_w1(nc.scalar.copy, 0, 0, 0)
-        quantize_w1_pass(0, 0, 0)
-        weave_w1(nc.scalar.copy, 0, 0, 1)
+        for g in range(2):
+            weave_w1(nc.scalar.copy, 0, 0, g)
+            quantize_w1_pass(0, 0, g)
+        load_w1(1, 1, "slot_c")
         weave_w1(nc.vector.tensor_copy, 1, 0, 0)
-        quantize_w1_pass(1, 0, 0)
         weave_w1(nc.scalar.copy, 1, 0, 1)
-        quantize_w1_pass(0, 0, 1)
-        quantize_w1_pass(1, 0, 1)
+        for g in range(2):
+            quantize_w1_pass(1, 0, g)
+        for j0 in range(0, S, BANK):
+            listed = offs_sb[:, j0 // 16 : (j0 + BANK) // 16]
+            nc.vector.tensor_copy(v_w[1][:, j0 : j0 + BANK], tab_w1[:].indirect(listed))
         w3_raw = []
         for b in range(HP):
             raw = sbuf([P, PACK, N], F32, f"w3_raw{b}", ("slot_d", "slot_a")[b])
             nc.sync.dma_start(raw[:], w3[PASS * b : PASS * (b + 1), :].rearrange("(p j) c -> p j c", j=PACK))
             w3_raw.append(raw)
 
-        bow0_f = sbuf([P, PACK, M], F32, "bow0_f")
-        st0_f = sbuf([P, PACK, M], F32, "st0_f")
+        gain_sb = sbuf([P, HP, PACK], F32, "gain_sb", "w1_bf00")
+        mid_sb = sbuf([P, HP, PACK], F32, "mid_sb", "w1_bf01")
+        nc.sync.dma_start(gain_sb[:], gain.rearrange("(b p t) -> p b t", b=HP, t=PACK))
+        nc.sync.dma_start(mid_sb[:], mid.rearrange("(b p t) -> p b t", b=HP, t=PACK))
+        nc.scalar.mul(minus_mid[:], mid_sb[:], -1.0)
+
+        def w3_part(copy, c):
+            b, n0 = divmod(W3_CHUNK * c, N)
+            weave(copy, w3_bf[:, PACK * W3_CHUNK * c : PACK * W3_CHUNK * (c + 1)], w3_raw[b][:, :, n0 : n0 + W3_CHUNK])
+
         for t in range(PACK):
-            act = sbuf([P, S], F32, f"act0{t}", f"act{t % 3}")
-            reading(0, t, act, nc.vector.tensor_scalar if t == 0 else nc.gpsimd.tensor_scalar)
-            pick(bow0_f, 0, t, pos1_sb[:])
-            pick(st0_f, 0, t, pos2_sb[:])
-            if t % 2 == 1:
-                both_passes_w1(1, t // 2)
+            if t == 0:
+                weave_w1(nc.vector.tensor_copy, 0, 1, 0)
+            if t == 2:
+                weave_w1(nc.scalar.copy, 0, 1, 1)
+                weave_w1(nc.scalar.copy, 1, 1, 0)
+                quantize_w1_both(1, 0)
+            reading(0, t)
+        weave_w1(nc.scalar.copy, 1, 1, 1)
+        quantize_w1_both(1, 1)
 
         w2_w = sbuf([P, HP, 2 * N], U8, "w2_w", "slot_c")
         w2_sc = sbuf([P, HP, N], U8, "w2_sc", "picked_sc")
@@ -193,87 +210,55 @@ def tile_list_towing_team_scores_kernel(
         cur_sb = sbuf([P, NT, M], F32, "cur_sb", "slot_b")
         nc.sync.dma_start(cur_sb[:], cur.rearrange("(i p) m -> p i m", p=P))
 
-        def offsets(pos_sb, u):
-            return pos_sb[:, HALF // 16 * u : HALF // 16 * (u + 1)]
-
-        bow1_f = sbuf([P, PACK, HALF], F32, "bow1_f")
-        st1_f = sbuf([P, PACK, HALF], F32, "st1_f")
+        chunks = HP * N // W3_CHUNK
+        for c in range(1):
+            w3_part(nc.scalar.copy, c)
         for t in range(PACK):
-            act = sbuf([P, S], F32, f"act1{t}", ("act1", "bow0_bf", "st0_bf", "bow2_f")[t])
-            reading(1, t, act, nc.gpsimd.tensor_scalar)
-            pick(bow1_f, 1, t, offsets(pos1_sb, 0))
-            pick(st1_f, 1, t, offsets(pos2_sb, 0))
-        weave_teams(nc.scalar.copy, bow0_f[:], bow_q[0][:], bow_sc[0][:], "bow0_bf")
-        weave_teams(scalar_abs, st0_f[:], st_q[0][:], st_sc[0][:], "st0_bf")
-        for c in range(HP * N // W3_CHUNK):
-            b, n0 = divmod(W3_CHUNK * c, N)
-            woven = w3_bf[:, PACK * W3_CHUNK * c : PACK * W3_CHUNK * (c + 1)]
-            nc.gpsimd.tensor_scalar(
-                woven.rearrange("p (n j) -> p n j", j=PACK),
-                w3_raw[b][:, :, n0 : n0 + W3_CHUNK].rearrange("p j n -> p n j"),
-                1.0, 0.0, ALU.mult, ALU.add,
-            )
+            reading(1, t)
+        rounded("bow", 0, range(PACK))
+        quantize_teams("bow", 0)
+        rounded("stern", 0, range(PACK))
+        quantize_teams("stern", 0)
+        for c in range(1, chunks):
+            w3_part(nc.scalar.copy if c < chunks - W3_ON_VECTOR else nc.vector.tensor_copy, c)
+            if c == 2:
+                rounded("bow", 1, range(PACK))
+                quantize_teams("bow", 1)
+                rounded("stern", 1, range(PACK))
+                quantize_teams("stern", 1)
         quantize(w3_q[:, :W3_SPLIT], w3_sc[:, :W3_SPLIT], w3_bf[:, : PACK * W3_SPLIT])
         quantize(w3_q[:, W3_SPLIT:], w3_sc[:, W3_SPLIT:], w3_bf[:, PACK * W3_SPLIT :])
-        bow2_f = sbuf([P, PACK, HALF], F32, "bow2_f")
-        for t in range(PACK):
-            pick(bow2_f, 1, t, offsets(pos1_sb, 1))
 
-        def bow_scores(u, banks):
-            for i0 in range(0, NT, 2):
-                acc = bank(banks[i0 // 2])
-                for b in range(HP):
-                    for e in range(2):
-                        i = i0 + e
-                        for m0 in range(0, HALF, QUARTER):
-                            teams = slice(HALF * u + m0, HALF * u + m0 + QUARTER)
-                            nc.tensor.matmul_mx(
-                                out=acc[:, HALF * e + m0 : HALF * e + m0 + QUARTER],
-                                lhsT=w2_w[:, b, 2 * P * i : 2 * P * (i + 1)].bitcast(FP4X4),
-                                lhsT_scale=w2_sc[:, b, P * i : P * (i + 1)],
-                                rhs=bow_q[b][:, teams].bitcast(FP8X4),
-                                rhs_scale=bow_sc[b][:, teams],
-                                start=(b == 0 and e == 0 and m0 == 0),
-                                stop=(b == HP - 1 and e == 1 and m0 == QUARTER),
-                            )
-                nc.scalar.copy(scores[u][i0 // 2][:], acc[:])
+        for i in range(NT):
+            acc = bank((4, 5, 6, 7, 0, 1)[i])
+            for b in range(HP):
+                nc.tensor.matmul_mx(
+                    out=acc[:],
+                    lhsT=w2_w[:, b, 2 * P * i : 2 * P * (i + 1)].bitcast(FP4X4),
+                    lhsT_scale=w2_sc[:, b, P * i : P * (i + 1)],
+                    rhs=team_q["bow", b][:].bitcast(FP8X4),
+                    rhs_scale=team_sc["bow", b][:],
+                    start=(b == 0),
+                    stop=(b == HP - 1),
+                )
+            nc.scalar.copy(scores[i][:], acc[:])
 
-        out_rows = out.rearrange("(i p) m -> p i m", p=P)
+        for i in range(NT):
+            acc = bank((2, 3, 4, 5, 6, 7)[i])
+            for b in range(HP):
+                cols = slice(N * b + P * i, N * b + P * (i + 1))
+                nc.tensor.matmul_mx(
+                    out=acc[:],
+                    lhsT=w3_q[:, cols].bitcast(FP8X4),
+                    lhsT_scale=w3_sc[:, cols],
+                    rhs=team_q["stern", b][:].bitcast(FP8X4),
+                    rhs_scale=team_sc["stern", b][:],
+                    start=(b == 0),
+                    stop=(b == HP - 1),
+                )
+            nc.vector.tensor_tensor(scores[i][:], acc[:], scores[i][:], ALU.min)
 
-        def finish(u, banks, subtract):
-            teams = slice(HALF * u, HALF * (u + 1))
-            for i0 in range(0, NT, 2):
-                acc = bank(banks[i0 // 2])
-                for b in range(HP):
-                    for e in range(2):
-                        cols = slice(N * b + P * (i0 + e), N * b + P * (i0 + e + 1))
-                        nc.tensor.matmul_mx(
-                            out=acc[:, HALF * e : HALF * (e + 1)],
-                            lhsT=w3_q[:, cols].bitcast(FP8X4),
-                            lhsT_scale=w3_sc[:, cols],
-                            rhs=st_q[b][:, teams].bitcast(FP8X4),
-                            rhs_scale=st_sc[b][:, teams],
-                            start=(b == 0 and e == 0),
-                            stop=(b == HP - 1 and e == 1),
-                        )
-                weaker = scores[u][i0 // 2][:]
-                nc.vector.tensor_tensor(weaker, acc[:], weaker, ALU.min)
-                res = weaker.rearrange("p (e m) -> p e m", e=2)
-                subtract(res, res, cur_sb[:, i0 : i0 + 2, teams], ALU.subtract)
-                nc.sync.dma_start(out_rows[:, i0 : i0 + 2, teams], res)
-
-        def weave_half(copy, picked, codes, scales, u, slot):
-            teams = slice(HALF * u, HALF * (u + 1))
-            weave_teams(copy, picked, codes[1][:, teams], scales[1][:, teams], slot)
-
-        weave_half(nc.scalar.copy, bow1_f[:], bow_q, bow_sc, 0, "bow1_bf")
-        weave_half(scalar_abs, st1_f[:], st_q, st_sc, 0, "st2_f")
-        st2_f = sbuf([P, PACK, HALF], F32, "st2_f")
-        for t in range(PACK):
-            pick(st2_f, 1, t, offsets(pos2_sb, 1))
-        weave_half(nc.scalar.copy, bow2_f[:], bow_q, bow_sc, 1, "bow2_bf")
-        bow_scores(0, (4, 5, 6))
-        weave_half(scalar_abs, st2_f[:], st_q, st_sc, 1, "st2_bf")
-        finish(0, (7, 0, 1), nc.gpsimd.tensor_tensor)
-        bow_scores(1, (2, 3, 4))
-        finish(1, (5, 6, 7), nc.vector.tensor_tensor)
+        for i in range(NT):
+            engine = nc.gpsimd if i < SUBTRACT_ON_GPSIMD else nc.vector
+            engine.tensor_tensor(scores[i][:], scores[i][:], cur_sb[:, i, :], ALU.subtract)
+            nc.sync.dma_start(out[P * i : P * (i + 1), :], scores[i][:])

@@ -20,14 +20,24 @@ P = 128
 PACK = 4
 PASS = P * PACK
 BANK = 512
-KP = K // PASS
-HP = H // PASS
-NT = N // P
-DEAD = 32 - 4 * KP
-W3_CHUNK = 256
-W3_ON_VECTOR = 1
-W3_SPLIT = 1024
+BANKS = 8
+QUAD = 32
+QUADS = P // QUAD
+BLOCK = 32
+QUAD_ROWS = 4
+LIST_ROWS = 16
+K_PASSES = K // PASS
+H_PASSES = H // PASS
+N_TILES = N // P
+SCALE_ROWS_AT = P - K // BLOCK
+ENDS = ("bow", "stern")
 STAGE1_BANKS = 4
+BOW_BANK0 = STAGE1_BANKS
+STERN_BANK0 = (BOW_BANK0 + N_TILES) % BANKS
+SILU_SLOTS = 4
+W3_CHUNK = 256
+W3_BEFORE_LAST_PLANES = 4
+W3_SPLIT = 1024
 SUBTRACT_ON_GPSIMD = 2
 
 
@@ -45,68 +55,59 @@ def tile_list_towing_team_scores_kernel(
         def bank(n):
             return psum.tile([P, BANK], F32, name=f"bank{n}")
 
-        offs_sb = keep.tile([P, S // 16], U16, name="offs_sb")
-        pos1_sb = keep.tile([P, M // 16], U16, name="pos1_sb")
-        pos2_sb = keep.tile([P, M // 16], U16, name="pos2_sb")
-        tab_sc = sbuf([P, T], U8, "tab_sc", "slot_a")
-        tab_w0 = sbuf([P, T], U16, "tab_w0", "slot_b")
-        picked_sc = sbuf([P, S], U8, "picked_sc")
-        v_w = [sbuf([P, S], U16, f"v_w{a}") for a in range(KP)]
-        v_sc = [sbuf([P, S], U8, f"v_sc{a}") for a in range(KP)]
-        w1_raw = {}
-        w1_bf = {(b, g): sbuf([P, KP, 2 * PASS], BF16, f"w1_bf{b}{g}") for b in range(HP) for g in range(2)}
-        w1_q = {(b, g): sbuf([P, KP, 2 * P], U32, f"w1_q{b}{g}") for b in range(HP) for g in range(2)}
-        w1_sc = {(b, g): sbuf([P, KP, 2 * P], U8, f"w1_sc{b}{g}") for b in range(HP) for g in range(2)}
-        w3_bf = sbuf([P, HP * N * PACK], BF16, "w3_bf")
-        w3_q = sbuf([P, HP * N], U32, "w3_q")
-        w3_sc = sbuf([P, HP * N], U8, "w3_sc")
-        minus_mid = sbuf([P, HP, PACK], F32, "minus_mid")
-        warm = sbuf([P, 8], F32, "warm")
-        warm_out = sbuf([P, 8], F32, "warm_out")
-        ends = ("bow", "stern")
-        lists = {"bow": pos1_sb, "stern": pos2_sb}
-        funcs = {"bow": ACT.Identity, "stern": ACT.Abs}
-        team_q = {(e, b): sbuf([P, M], U32, f"{e}_q{b}") for e in ends for b in range(HP)}
-        team_sc = {(e, b): sbuf([P, M], U8, f"{e}_sc{b}") for e in ends for b in range(HP)}
-        planes = {}
-        picked = {}
-        scores = [sbuf([P, M], F32, f"scores{i}") for i in range(NT)]
+        def quantize(codes, scales, values):
+            nc.vector.quantize_mx(out=codes.bitcast(FP8X4), scales=scales, in_=values)
 
-        nc.gpsimd.memset(warm[:], 0.0)
-        for q in range(4):
-            engine = nc.vector if q < 2 else nc.gpsimd
-            engine.memset(tab_sc[32 * q : 32 * q + DEAD, :].bitcast(I32), 0)
-        nc.scalar.activation(warm_out[:], warm[:], ACT.Silu)
+        def weave(copy, dst, src):
+            copy(
+                dst.rearrange("p (c i t) -> p c t i", i=PACK, t=PACK),
+                src.rearrange("p t (c i) -> p c t i", i=PACK),
+            )
+
+        offs_sb = keep.tile([P, S // LIST_ROWS], U16, name="offs_sb")
+        team_list = {e: keep.tile([P, M // LIST_ROWS], U16, name=f"{e}_list") for e in ENDS}
+        tab_sc = sbuf([P, T], U8, "tab_sc", "slot_a")
+        tab_w = [sbuf([P, T], U16, f"tab_w{a}", slot) for a, slot in enumerate(("slot_b", "slot_c"))]
+
+        nc.vector.memset(tab_sc[0:SCALE_ROWS_AT, :].bitcast(I32), 0)
 
         nc.sync.dma_start(offs_sb[:], offs)
-        for q in range(4):
-            nc.sync.dma_start(
-                tab_sc[32 * q + DEAD : 32 * (q + 1), :].bitcast(I32),
-                tab_scales[:, 4 * q : 4 * q + 4, :].bitcast(I32),
-            )
-        nc.sync.dma_start(tab_w0[:].bitcast(I32), tab_words[0].bitcast(I32))
+        nc.sync.dma_start(team_list["bow"][:], pos1)
+        nc.sync.dma_start(team_list["stern"][:], pos2)
+        nc.sync.dma_start(
+            tab_sc[SCALE_ROWS_AT:P, :].bitcast(I32), tab_scales.rearrange("a g c -> g a c").bitcast(I32)
+        )
+        for a in range(K_PASSES):
+            nc.sync.dma_start(tab_w[a][:].bitcast(I32), tab_words[a].bitcast(I32))
+
+        w1_raw = {}
 
         def load_w1(a, b, slot):
             w1_raw[a, b] = sbuf([P, PACK, PASS], F32, f"w1_raw{a}{b}", slot)
             rows = w1[PASS * a : PASS * (a + 1), PASS * b : PASS * (b + 1)]
             nc.sync.dma_start(w1_raw[a, b][:], rows.rearrange("(p j) c -> p j c", j=PACK))
 
-        load_w1(0, 0, "slot_c")
-        load_w1(1, 0, "slot_d")
-        nc.sync.dma_start(pos1_sb[:], pos1)
-        nc.sync.dma_start(pos2_sb[:], pos2)
+        load_w1(0, 0, "slot_d")
 
+        picked_sc = sbuf([P, S], U8, "picked_sc")
+        v_sc = sbuf([P, K_PASSES, S], U8, "v_sc")
+        v_w = [sbuf([P, S], U16, f"v_w{a}") for a in range(K_PASSES)]
         nc.vector.tensor_copy(picked_sc[:], tab_sc[:].indirect(offs_sb[:]))
-        for a in range(KP):
-            first = DEAD + 4 * a
-            nc.sync.dma_start(v_sc[a][0 : P - first, :].bitcast(I32), picked_sc[first:P, :].bitcast(I32))
-        tab_w1 = sbuf([P, T], U16, "tab_w1", "slot_a")
-        nc.sync.dma_start(tab_w1[:].bitcast(I32), tab_words[1].bitcast(I32))
-        nc.vector.tensor_copy(v_w[0][:], tab_w0[:].indirect(offs_sb[:]))
-        load_w1(0, 1, "slot_b")
+        for q in range(QUADS):
+            first = SCALE_ROWS_AT + K_PASSES * QUAD_ROWS * q
+            nc.sync.dma_start(
+                v_sc[QUAD * q : QUAD * q + QUAD_ROWS, :, :].bitcast(I32),
+                picked_sc[first : first + K_PASSES * QUAD_ROWS, :].bitcast(I32),
+            )
+        load_w1(1, 0, "slot_a")
+        for a, slot in enumerate(("slot_b", "slot_c")):
+            nc.vector.tensor_copy(v_w[a][:], tab_w[a][:].indirect(offs_sb[:]))
+            load_w1(a, 1, slot)
 
-        def quantize(codes, scales, values):
-            nc.vector.quantize_mx(out=codes.bitcast(FP8X4), scales=scales, in_=values)
+        pairs = [(b, g) for b in range(H_PASSES) for g in range(PACK // 2)]
+        w1_bf = {(b, g): sbuf([P, K_PASSES, 2 * PASS], BF16, f"w1_bf{b}{g}") for b, g in pairs}
+        w1_q = {(b, g): sbuf([P, K_PASSES, 2 * P], U32, f"w1_q{b}{g}") for b, g in pairs}
+        w1_sc = {(b, g): sbuf([P, K_PASSES, 2 * P], U8, f"w1_sc{b}{g}") for b, g in pairs}
 
         def weave_w1(copy, a, b, g):
             dst = w1_bf[b, g][:, a, :].rearrange("p (t m j) -> p m j t", m=P, j=PACK)
@@ -116,149 +117,152 @@ def tile_list_towing_team_scores_kernel(
         def quantize_w1_pass(a, b, g):
             quantize(w1_q[b, g][:, a, :], w1_sc[b, g][:, a, :], w1_bf[b, g][:, a, :])
 
-        def quantize_w1_both(b, g):
+        def quantize_w1_pair(b, g):
             flat = "p a c -> p (a c)"
             quantize(w1_q[b, g][:].rearrange(flat), w1_sc[b, g][:].rearrange(flat), w1_bf[b, g][:].rearrange(flat))
 
-        def weave(copy, dst, src):
-            copy(
-                dst.rearrange("p (c i j) -> p c j i", i=PACK, j=PACK),
-                src.rearrange("p j (c i) -> p c j i", i=PACK),
-            )
+        weave_w1(nc.scalar.copy, 0, 0, 0)
+        quantize_w1_pass(0, 0, 0)
+        weave_w1(nc.scalar.copy, 0, 0, 1)
+        weave_w1(nc.vector.tensor_copy, 1, 0, 0)
+        quantize_w1_pass(1, 0, 0)
+        weave_w1(nc.vector.tensor_copy, 1, 0, 1)
+        quantize_w1_pair(0, 1)
 
-        def reading(b, t):
+        w3_raw = []
+        for b, slot in enumerate(("slot_d", "slot_a")):
+            w3_raw.append(sbuf([P, PACK, N], F32, f"w3_raw{b}", slot))
+            rows = w3[PASS * b : PASS * (b + 1), :]
+            nc.sync.dma_start(w3_raw[b][:], rows.rearrange("(p j) c -> p j c", j=PACK))
+        gain_sb = sbuf([P, H_PASSES, PACK], F32, "gain_sb", "w1_bf00")
+        mid_sb = sbuf([P, H_PASSES, PACK], F32, "mid_sb", "w1_bf01")
+        minus_mid = sbuf([P, H_PASSES, PACK], F32, "minus_mid")
+        nc.sync.dma_start(gain_sb[:], gain.rearrange("(b p t) -> p b t", b=H_PASSES, t=PACK))
+        nc.sync.dma_start(mid_sb[:], mid.rearrange("(b p t) -> p b t", b=H_PASSES, t=PACK))
+        nc.scalar.mul(minus_mid[:], mid_sb[:], -1.0)
+
+        picked = {}
+
+        def read_and_pick(b, t):
             g, cols = t // 2, slice(P * (t % 2), P * (t % 2 + 1))
-            act = sbuf([P, S], F32, f"act{b}{t}", f"act{(PACK * b + t) % 4}")
+            silu = sbuf([P, S], F32, f"silu{b}{t}", f"silu{(PACK * b + t) % SILU_SLOTS}")
             for jb in range(S // BANK):
                 listed = slice(BANK * jb, BANK * (jb + 1))
-                acc = bank((2 * t + jb) % STAGE1_BANKS)
-                for a in range(KP):
+                acc = bank((S // BANK * t + jb) % STAGE1_BANKS)
+                for a in range(K_PASSES):
                     nc.tensor.matmul_mx(
                         out=acc[:],
                         lhsT=w1_q[b, g][:, a, cols].bitcast(FP8X4),
                         lhsT_scale=w1_sc[b, g][:, a, cols],
                         rhs=v_w[a][:, listed].bitcast(FP4X4),
-                        rhs_scale=v_sc[a][:, listed],
+                        rhs_scale=v_sc[:, a, listed],
                         start=(a == 0),
-                        stop=(a == KP - 1),
+                        stop=(a == K_PASSES - 1),
                     )
-                nc.scalar.activation(act[:, listed], acc[:], ACT.Silu)
-            for e in ends:
+                nc.scalar.activation(silu[:, listed], acc[:], ACT.Silu)
+            for e in ENDS:
                 slot = "w1_bf10" if (e, b, t) == ("stern", 0, 2) else ""
                 picked[e, b, t] = sbuf([P, M], F32, f"{e}_picked{b}{t}", slot)
-                nc.vector.tensor_copy(picked[e, b, t][:], act[:].indirect(lists[e][:]))
+                nc.vector.tensor_copy(picked[e, b, t][:], silu[:].indirect(team_list[e][:]))
 
-        def rounded(e, b, ts):
-            planes[e, b] = sbuf([P, PACK, M], BF16, f"{e}_planes{b}", f"act{ends.index(e)}" if b == 0 else "")
-            for t in ts:
-                nc.scalar.activation(
-                    planes[e, b][:, t, :], picked[e, b, t][:], funcs[e],
-                    bias=minus_mid[:, b, t : t + 1], scale=gain_sb[:, b, t : t + 1],
-                )
-
-        def quantize_teams(e, b, slot=""):
-            woven = sbuf([P, M * PACK], BF16, f"{e}_woven{b}", slot)
-            weave(nc.vector.tensor_copy, woven[:], planes[e, b][:])
-            quantize(team_q[e, b][:], team_sc[e, b][:], woven[:])
-
-        for g in range(2):
-            weave_w1(nc.scalar.copy, 0, 0, g)
-            quantize_w1_pass(0, 0, g)
-        load_w1(1, 1, "slot_c")
-        weave_w1(nc.vector.tensor_copy, 1, 0, 0)
-        weave_w1(nc.scalar.copy, 1, 0, 1)
-        for g in range(2):
-            quantize_w1_pass(1, 0, g)
-        for j0 in range(0, S, BANK):
-            listed = offs_sb[:, j0 // 16 : (j0 + BANK) // 16]
-            nc.vector.tensor_copy(v_w[1][:, j0 : j0 + BANK], tab_w1[:].indirect(listed))
-        w3_raw = []
-        for b in range(HP):
-            raw = sbuf([P, PACK, N], F32, f"w3_raw{b}", ("slot_d", "slot_a")[b])
-            nc.sync.dma_start(raw[:], w3[PASS * b : PASS * (b + 1), :].rearrange("(p j) c -> p j c", j=PACK))
-            w3_raw.append(raw)
-
-        gain_sb = sbuf([P, HP, PACK], F32, "gain_sb", "w1_bf00")
-        mid_sb = sbuf([P, HP, PACK], F32, "mid_sb", "w1_bf01")
-        nc.sync.dma_start(gain_sb[:], gain.rearrange("(b p t) -> p b t", b=HP, t=PACK))
-        nc.sync.dma_start(mid_sb[:], mid.rearrange("(b p t) -> p b t", b=HP, t=PACK))
-        nc.scalar.mul(minus_mid[:], mid_sb[:], -1.0)
-
-        def w3_part(copy, c):
-            b, n0 = divmod(W3_CHUNK * c, N)
-            weave(copy, w3_bf[:, PACK * W3_CHUNK * c : PACK * W3_CHUNK * (c + 1)], w3_raw[b][:, :, n0 : n0 + W3_CHUNK])
-
-        for t in range(PACK):
-            if t == 0:
-                weave_w1(nc.vector.tensor_copy, 0, 1, 0)
-            if t == 2:
-                weave_w1(nc.scalar.copy, 0, 1, 1)
-                weave_w1(nc.scalar.copy, 1, 1, 0)
-                quantize_w1_both(1, 0)
-            reading(0, t)
+        weave_w1(nc.vector.tensor_copy, 0, 1, 0)
+        read_and_pick(0, 0)
+        read_and_pick(0, 1)
+        weave_w1(nc.scalar.copy, 0, 1, 1)
+        weave_w1(nc.scalar.copy, 1, 1, 0)
+        quantize_w1_pair(1, 0)
+        read_and_pick(0, 2)
+        read_and_pick(0, 3)
         weave_w1(nc.scalar.copy, 1, 1, 1)
-        quantize_w1_both(1, 1)
+        quantize_w1_pair(1, 1)
 
-        w2_w = sbuf([P, HP, 2 * N], U8, "w2_w", "slot_c")
-        w2_sc = sbuf([P, HP, N], U8, "w2_sc", "picked_sc")
+        w2_w = sbuf([P, H_PASSES, 2 * N], U8, "w2_w", "slot_c")
+        w2_sc = sbuf([P, H_PASSES, N], U8, "w2_sc", "w1_bf11")
+        cur_sb = sbuf([P, N_TILES, M], F32, "cur_sb", "slot_b")
         nc.sync.dma_start(w2_w[:].bitcast(I32), w2_words.rearrange("b p c -> p b c").bitcast(I32))
-        for q in range(4):
-            nc.sync.dma_start(
-                w2_sc[32 * q : 32 * q + 4, :, :].bitcast(I32),
-                w2_scales[:, 4 * q : 4 * q + 4, :].rearrange("b r c -> r b c").bitcast(I32),
-            )
-        cur_sb = sbuf([P, NT, M], F32, "cur_sb", "slot_b")
+        for q in range(QUADS):
+            rows = w2_scales[:, QUAD_ROWS * q : QUAD_ROWS * (q + 1), :]
+            live = w2_sc[QUAD * q : QUAD * q + QUAD_ROWS, :, :]
+            nc.sync.dma_start(live.bitcast(I32), rows.rearrange("b r c -> r b c").bitcast(I32))
         nc.sync.dma_start(cur_sb[:], cur.rearrange("(i p) m -> p i m", p=P))
 
-        chunks = HP * N // W3_CHUNK
-        for c in range(1):
-            w3_part(nc.scalar.copy, c)
+        w3_bf = sbuf([P, H_PASSES * N * PACK], BF16, "w3_bf")
+        w3_q = sbuf([P, H_PASSES * N], U32, "w3_q")
+        w3_sc = sbuf([P, H_PASSES * N], U8, "w3_sc")
+        w3_chunks = H_PASSES * N // W3_CHUNK
+
+        def weave_w3(c):
+            b, n0 = divmod(W3_CHUNK * c, N)
+            woven = w3_bf[:, PACK * W3_CHUNK * c : PACK * W3_CHUNK * (c + 1)]
+            weave(nc.scalar.copy, woven, w3_raw[b][:, :, n0 : n0 + W3_CHUNK])
+
         for t in range(PACK):
-            reading(1, t)
-        rounded("bow", 0, range(PACK))
-        quantize_teams("bow", 0)
-        rounded("stern", 0, range(PACK))
-        quantize_teams("stern", 0)
-        for c in range(1, chunks):
-            w3_part(nc.scalar.copy if c < chunks - W3_ON_VECTOR else nc.vector.tensor_copy, c)
-            if c == 2:
-                rounded("bow", 1, range(PACK))
-                quantize_teams("bow", 1)
-                rounded("stern", 1, range(PACK))
-                quantize_teams("stern", 1)
+            if t % 2 == 0:
+                weave_w3(t // 2)
+            read_and_pick(1, t)
+
+        team_bf = [sbuf([P, len(ENDS), M * PACK], BF16, f"team_bf{b}") for b in range(H_PASSES)]
+        team_q = [sbuf([P, len(ENDS), M], U32, f"team_q{b}") for b in range(H_PASSES)]
+        team_sc = [sbuf([P, len(ENDS), M], U8, f"team_sc{b}") for b in range(H_PASSES)]
+
+        def round_and_weave(e, b):
+            side = ENDS.index(e)
+            planes = sbuf([P, PACK, M], BF16, f"{e}_planes{b}", f"silu{side}" if b == 0 else "")
+            for t in range(PACK):
+                nc.scalar.activation(
+                    planes[:, t, :],
+                    picked[e, b, t][:],
+                    ACT.Identity if e == "bow" else ACT.Abs,
+                    bias=minus_mid[:, b, t : t + 1],
+                    scale=gain_sb[:, b, t : t + 1],
+                )
+            weave(nc.vector.tensor_copy, team_bf[b][:, side, :], planes[:])
+
+        for e in ENDS:
+            round_and_weave(e, 0)
+        both = "p e c -> p (e c)"
+        quantize(team_q[0][:].rearrange(both), team_sc[0][:].rearrange(both), team_bf[0][:].rearrange(both))
+        for c in range(PACK // 2, W3_BEFORE_LAST_PLANES):
+            weave_w3(c)
+        for side, e in enumerate(ENDS):
+            round_and_weave(e, 1)
+            quantize(team_q[1][:, side, :], team_sc[1][:, side, :], team_bf[1][:, side, :])
+        for c in range(W3_BEFORE_LAST_PLANES, w3_chunks):
+            weave_w3(c)
         quantize(w3_q[:, :W3_SPLIT], w3_sc[:, :W3_SPLIT], w3_bf[:, : PACK * W3_SPLIT])
         quantize(w3_q[:, W3_SPLIT:], w3_sc[:, W3_SPLIT:], w3_bf[:, PACK * W3_SPLIT :])
 
-        for i in range(NT):
-            acc = bank((4, 5, 6, 7, 0, 1)[i])
-            for b in range(HP):
+        scores = [sbuf([P, M], F32, f"scores{i}") for i in range(N_TILES)]
+        for i in range(N_TILES):
+            acc = bank((BOW_BANK0 + i) % BANKS)
+            for b in range(H_PASSES):
                 nc.tensor.matmul_mx(
                     out=acc[:],
                     lhsT=w2_w[:, b, 2 * P * i : 2 * P * (i + 1)].bitcast(FP4X4),
                     lhsT_scale=w2_sc[:, b, P * i : P * (i + 1)],
-                    rhs=team_q["bow", b][:].bitcast(FP8X4),
-                    rhs_scale=team_sc["bow", b][:],
+                    rhs=team_q[b][:, 0, :].bitcast(FP8X4),
+                    rhs_scale=team_sc[b][:, 0, :],
                     start=(b == 0),
-                    stop=(b == HP - 1),
+                    stop=(b == H_PASSES - 1),
                 )
             nc.scalar.copy(scores[i][:], acc[:])
 
-        for i in range(NT):
-            acc = bank((2, 3, 4, 5, 6, 7)[i])
-            for b in range(HP):
+        for i in range(N_TILES):
+            acc = bank((STERN_BANK0 + i) % BANKS)
+            for b in range(H_PASSES):
                 cols = slice(N * b + P * i, N * b + P * (i + 1))
                 nc.tensor.matmul_mx(
                     out=acc[:],
                     lhsT=w3_q[:, cols].bitcast(FP8X4),
                     lhsT_scale=w3_sc[:, cols],
-                    rhs=team_q["stern", b][:].bitcast(FP8X4),
-                    rhs_scale=team_sc["stern", b][:],
+                    rhs=team_q[b][:, 1, :].bitcast(FP8X4),
+                    rhs_scale=team_sc[b][:, 1, :],
                     start=(b == 0),
-                    stop=(b == HP - 1),
+                    stop=(b == H_PASSES - 1),
                 )
             nc.vector.tensor_tensor(scores[i][:], acc[:], scores[i][:], ALU.min)
 
-        for i in range(NT):
+        for i in range(N_TILES):
             engine = nc.gpsimd if i < SUBTRACT_ON_GPSIMD else nc.vector
             engine.tensor_tensor(scores[i][:], scores[i][:], cur_sb[:, i, :], ALU.subtract)
             nc.sync.dma_start(out[P * i : P * (i + 1), :], scores[i][:])

from contextlib import ExitStack

import concourse.mybir as mybir

K, T, S, H, N, M = 1024, 4096, 1024, 1024, 768, 512
FLOPS = 2 * K * H * S + 2 * 2 * H * N * M

F32 = mybir.dt.float32
BF16 = mybir.dt.bfloat16
I32 = mybir.dt.int32
U32 = mybir.dt.uint32
U16 = mybir.dt.uint16
U8 = mybir.dt.uint8
FP8X4 = mybir.dt.float8_e4m3fn_x4
FP4X4 = mybir.dt.float4_e2m1fn_x4
ACT = mybir.ActivationFunctionType
ALU = mybir.AluOpType

P = 128
PACK = 4
PASS = P * PACK
BANK = 512
BANKS = 8
QUAD = 32
QUADS = P // QUAD
BLOCK = 32
QUAD_ROWS = 4
LIST_ROWS = 16
K_PASSES = K // PASS
H_PASSES = H // PASS
N_TILES = N // P
SCALE_ROWS_AT = P - K // BLOCK
ENDS = ("bow", "stern")
STAGE1_BANKS = 4
BOW_BANK0 = STAGE1_BANKS
STERN_BANK0 = (BOW_BANK0 + N_TILES) % BANKS
SILU_SLOTS = 4
W3_CHUNK = 256
W3_BEFORE_LAST_PLANES = 4
W3_SPLIT = 1024
SUBTRACT_ON_GPSIMD = 2


def tile_list_towing_team_scores_kernel(
    tc, tab_words, tab_scales, offs, w1, gain, mid, pos1, pos2, w2_words, w2_scales, w3, cur, out
):
    nc = tc.nc
    with ExitStack() as ctx:
        keep = ctx.enter_context(tc.tile_pool(name="keep", bufs=1))
        psum = ctx.enter_context(tc.psum_pool(name="psum", bufs=1))

        def sbuf(shape, dtype, name, slot=""):
            return keep.tile(shape, dtype, name=name, tag=slot, align_bytes=64)

        def bank(n):
            return psum.tile([P, BANK], F32, name=f"bank{n}")

        def quantize(codes, scales, values):
            nc.vector.quantize_mx(out=codes.bitcast(FP8X4), scales=scales, in_=values)

        def weave(copy, dst, src):
            copy(
                dst.rearrange("p (c i t) -> p c t i", i=PACK, t=PACK),
                src.rearrange("p t (c i) -> p c t i", i=PACK),
            )

        offs_sb = keep.tile([P, S // LIST_ROWS], U16, name="offs_sb")
        team_list = {e: keep.tile([P, M // LIST_ROWS], U16, name=f"{e}_list") for e in ENDS}
        tab_sc = sbuf([P, T], U8, "tab_sc", "slot_a")
        tab_w = [sbuf([P, T], U16, f"tab_w{a}", slot) for a, slot in enumerate(("slot_b", "slot_c"))]

        nc.vector.memset(tab_sc[0:SCALE_ROWS_AT, :].bitcast(I32), 0)

        nc.sync.dma_start(offs_sb[:], offs)
        nc.sync.dma_start(team_list["bow"][:], pos1)
        nc.sync.dma_start(team_list["stern"][:], pos2)
        nc.sync.dma_start(
            tab_sc[SCALE_ROWS_AT:P, :].bitcast(I32), tab_scales.rearrange("a g c -> g a c").bitcast(I32)
        )
        for a in range(K_PASSES):
            nc.sync.dma_start(tab_w[a][:].bitcast(I32), tab_words[a].bitcast(I32))

        w1_raw = {}

        def load_w1(a, b, slot):
            w1_raw[a, b] = sbuf([P, PACK, PASS], F32, f"w1_raw{a}{b}", slot)
            rows = w1[PASS * a : PASS * (a + 1), PASS * b : PASS * (b + 1)]
            nc.sync.dma_start(w1_raw[a, b][:], rows.rearrange("(p j) c -> p j c", j=PACK))

        load_w1(0, 0, "slot_d")

        picked_sc = sbuf([P, S], U8, "picked_sc")
        v_sc = sbuf([P, K_PASSES, S], U8, "v_sc")
        v_w = [sbuf([P, S], U16, f"v_w{a}") for a in range(K_PASSES)]
        nc.vector.tensor_copy(picked_sc[:], tab_sc[:].indirect(offs_sb[:]))
        for q in range(QUADS):
            first = SCALE_ROWS_AT + K_PASSES * QUAD_ROWS * q
            nc.sync.dma_start(
                v_sc[QUAD * q : QUAD * q + QUAD_ROWS, :, :].bitcast(I32),
                picked_sc[first : first + K_PASSES * QUAD_ROWS, :].bitcast(I32),
            )
        load_w1(1, 0, "slot_a")
        for a, slot in enumerate(("slot_b", "slot_c")):
            nc.vector.tensor_copy(v_w[a][:], tab_w[a][:].indirect(offs_sb[:]))
            load_w1(a, 1, slot)

        pairs = [(b, g) for b in range(H_PASSES) for g in range(PACK // 2)]
        w1_bf = {(b, g): sbuf([P, K_PASSES, 2 * PASS], BF16, f"w1_bf{b}{g}") for b, g in pairs}
        w1_q = {(b, g): sbuf([P, K_PASSES, 2 * P], U32, f"w1_q{b}{g}") for b, g in pairs}
        w1_sc = {(b, g): sbuf([P, K_PASSES, 2 * P], U8, f"w1_sc{b}{g}") for b, g in pairs}

        def weave_w1(copy, a, b, g):
            dst = w1_bf[b, g][:, a, :].rearrange("p (t m j) -> p m j t", m=P, j=PACK)
            src = w1_raw[a, b][:].rearrange("p j (m t) -> p m j t", t=PACK)
            copy(dst, src[:, :, :, 2 * g : 2 * g + 2])

        def quantize_w1_pass(a, b, g):
            quantize(w1_q[b, g][:, a, :], w1_sc[b, g][:, a, :], w1_bf[b, g][:, a, :])

        def quantize_w1_pair(b, g):
            flat = "p a c -> p (a c)"
            quantize(w1_q[b, g][:].rearrange(flat), w1_sc[b, g][:].rearrange(flat), w1_bf[b, g][:].rearrange(flat))

        weave_w1(nc.scalar.copy, 0, 0, 0)
        quantize_w1_pass(0, 0, 0)
        weave_w1(nc.scalar.copy, 0, 0, 1)
        weave_w1(nc.vector.tensor_copy, 1, 0, 0)
        quantize_w1_pass(1, 0, 0)
        weave_w1(nc.vector.tensor_copy, 1, 0, 1)
        quantize_w1_pair(0, 1)

        w3_raw = []
        for b, slot in enumerate(("slot_d", "slot_a")):
            w3_raw.append(sbuf([P, PACK, N], F32, f"w3_raw{b}", slot))
            rows = w3[PASS * b : PASS * (b + 1), :]
            nc.sync.dma_start(w3_raw[b][:], rows.rearrange("(p j) c -> p j c", j=PACK))
        gain_sb = sbuf([P, H_PASSES, PACK], F32, "gain_sb", "w1_bf00")
        mid_sb = sbuf([P, H_PASSES, PACK], F32, "mid_sb", "w1_bf01")
        minus_mid = sbuf([P, H_PASSES, PACK], F32, "minus_mid")
        nc.sync.dma_start(gain_sb[:], gain.rearrange("(b p t) -> p b t", b=H_PASSES, t=PACK))
        nc.sync.dma_start(mid_sb[:], mid.rearrange("(b p t) -> p b t", b=H_PASSES, t=PACK))
        nc.scalar.mul(minus_mid[:], mid_sb[:], -1.0)

        picked = {}

        def read_and_pick(b, t):
            g, cols = t // 2, slice(P * (t % 2), P * (t % 2 + 1))
            silu = sbuf([P, S], F32, f"silu{b}{t}", f"silu{(PACK * b + t) % SILU_SLOTS}")
            for jb in range(S // BANK):
                listed = slice(BANK * jb, BANK * (jb + 1))
                acc = bank((S // BANK * t + jb) % STAGE1_BANKS)
                for a in range(K_PASSES):
                    nc.tensor.matmul_mx(
                        out=acc[:],
                        lhsT=w1_q[b, g][:, a, cols].bitcast(FP8X4),
                        lhsT_scale=w1_sc[b, g][:, a, cols],
                        rhs=v_w[a][:, listed].bitcast(FP4X4),
                        rhs_scale=v_sc[:, a, listed],
                        start=(a == 0),
                        stop=(a == K_PASSES - 1),
                    )
                nc.scalar.activation(silu[:, listed], acc[:], ACT.Silu)
            for e in ENDS:
                slot = "w1_bf10" if (e, b, t) == ("stern", 0, 2) else ""
                picked[e, b, t] = sbuf([P, M], F32, f"{e}_picked{b}{t}", slot)
                nc.vector.tensor_copy(picked[e, b, t][:], silu[:].indirect(team_list[e][:]))

        weave_w1(nc.vector.tensor_copy, 0, 1, 0)
        read_and_pick(0, 0)
        read_and_pick(0, 1)
        weave_w1(nc.scalar.copy, 0, 1, 1)
        weave_w1(nc.scalar.copy, 1, 1, 0)
        quantize_w1_pair(1, 0)
        read_and_pick(0, 2)
        read_and_pick(0, 3)
        weave_w1(nc.scalar.copy, 1, 1, 1)
        quantize_w1_pair(1, 1)

        w2_w = sbuf([P, H_PASSES, 2 * N], U8, "w2_w", "slot_c")
        w2_sc = sbuf([P, H_PASSES, N], U8, "w2_sc", "w1_bf11")
        cur_sb = sbuf([P, N_TILES, M], F32, "cur_sb", "slot_b")
        nc.sync.dma_start(w2_w[:].bitcast(I32), w2_words.rearrange("b p c -> p b c").bitcast(I32))
        for q in range(QUADS):
            rows = w2_scales[:, QUAD_ROWS * q : QUAD_ROWS * (q + 1), :]
            live = w2_sc[QUAD * q : QUAD * q + QUAD_ROWS, :, :]
            nc.sync.dma_start(live.bitcast(I32), rows.rearrange("b r c -> r b c").bitcast(I32))
        nc.sync.dma_start(cur_sb[:], cur.rearrange("(i p) m -> p i m", p=P))

        w3_bf = sbuf([P, H_PASSES * N * PACK], BF16, "w3_bf")
        w3_q = sbuf([P, H_PASSES * N], U32, "w3_q")
        w3_sc = sbuf([P, H_PASSES * N], U8, "w3_sc")
        w3_chunks = H_PASSES * N // W3_CHUNK

        def weave_w3(c):
            b, n0 = divmod(W3_CHUNK * c, N)
            woven = w3_bf[:, PACK * W3_CHUNK * c : PACK * W3_CHUNK * (c + 1)]
            weave(nc.scalar.copy, woven, w3_raw[b][:, :, n0 : n0 + W3_CHUNK])

        for t in range(PACK):
            if t % 2 == 0:
                weave_w3(t // 2)
            read_and_pick(1, t)

        team_bf = [sbuf([P, len(ENDS), M * PACK], BF16, f"team_bf{b}") for b in range(H_PASSES)]
        team_q = [sbuf([P, len(ENDS), M], U32, f"team_q{b}") for b in range(H_PASSES)]
        team_sc = [sbuf([P, len(ENDS), M], U8, f"team_sc{b}") for b in range(H_PASSES)]

        def round_and_weave(e, b):
            side = ENDS.index(e)
            planes = sbuf([P, PACK, M], BF16, f"{e}_planes{b}", f"silu{side}" if b == 0 else "")
            for t in range(PACK):
                nc.scalar.activation(
                    planes[:, t, :],
                    picked[e, b, t][:],
                    ACT.Identity if e == "bow" else ACT.Abs,
                    bias=minus_mid[:, b, t : t + 1],
                    scale=gain_sb[:, b, t : t + 1],
                )
            weave(nc.vector.tensor_copy, team_bf[b][:, side, :], planes[:])

        for e in ENDS:
            round_and_weave(e, 0)
        both = "p e c -> p (e c)"
        quantize(team_q[0][:].rearrange(both), team_sc[0][:].rearrange(both), team_bf[0][:].rearrange(both))
        for c in range(PACK // 2, W3_BEFORE_LAST_PLANES):
            weave_w3(c)
        for side, e in enumerate(ENDS):
            round_and_weave(e, 1)
            quantize(team_q[1][:, side, :], team_sc[1][:, side, :], team_bf[1][:, side, :])
        for c in range(W3_BEFORE_LAST_PLANES, w3_chunks):
            weave_w3(c)
        quantize(w3_q[:, :W3_SPLIT], w3_sc[:, :W3_SPLIT], w3_bf[:, : PACK * W3_SPLIT])
        quantize(w3_q[:, W3_SPLIT:], w3_sc[:, W3_SPLIT:], w3_bf[:, PACK * W3_SPLIT :])

        scores = [sbuf([P, M], F32, f"scores{i}") for i in range(N_TILES)]
        for i in range(N_TILES):
            acc = bank((BOW_BANK0 + i) % BANKS)
            for b in range(H_PASSES):
                nc.tensor.matmul_mx(
                    out=acc[:],
                    lhsT=w2_w[:, b, 2 * P * i : 2 * P * (i + 1)].bitcast(FP4X4),
                    lhsT_scale=w2_sc[:, b, P * i : P * (i + 1)],
                    rhs=team_q[b][:, 0, :].bitcast(FP8X4),
                    rhs_scale=team_sc[b][:, 0, :],
                    start=(b == 0),
                    stop=(b == H_PASSES - 1),
                )
            nc.scalar.copy(scores[i][:], acc[:])

        for i in range(N_TILES):
            acc = bank((STERN_BANK0 + i) % BANKS)
            for b in range(H_PASSES):
                cols = slice(N * b + P * i, N * b + P * (i + 1))
                nc.tensor.matmul_mx(
                    out=acc[:],
                    lhsT=w3_q[:, cols].bitcast(FP8X4),
                    lhsT_scale=w3_sc[:, cols],
                    rhs=team_q[b][:, 1, :].bitcast(FP8X4),
                    rhs_scale=team_sc[b][:, 1, :],
                    start=(b == 0),
                    stop=(b == H_PASSES - 1),
                )
            nc.vector.tensor_tensor(scores[i][:], acc[:], scores[i][:], ALU.min)

        for i in range(N_TILES):
            engine = nc.gpsimd if i < SUBTRACT_ON_GPSIMD else nc.vector
            engine.tensor_tensor(scores[i][:], scores[i][:], cur_sb[:, i, :], ALU.subtract)
            nc.sync.dma_start(out[P * i : P * (i + 1), :], scores[i][:])
